import numpy as np, ml_dtypes
CORES = [9,25,41,57]
N = 4
import mx_ref
BF = ml_dtypes.bfloat16
def gentries(a):
    return np.ascontiguousarray(a.reshape(8, 16, -1).transpose(0, 2, 1)).reshape(8, -1)
def gtable(e):
    e = np.asarray(e); return np.ascontiguousarray(e.reshape(8, -1, 16).transpose(0, 2, 1)).reshape(128, -1).astype(np.int32)
def gcols(t, e):
    v = np.concatenate([t.reshape(8, 16, -1, 4), np.zeros((8, 16, 1, 4), BF)], axis=2)
    return np.ascontiguousarray(np.stack([v[g][:, e[g]] for g in range(8)])).reshape(128, -1)
def tile(rs):
    return np.stack(rs, axis=2).reshape(128, -1).astype(BF)
def pick(q, e):
    c = np.concatenate([q[0].reshape(128, -1, 4), np.zeros((128, 1, 4), np.uint8)], axis=1); s = np.concatenate([q[1], np.ones((16, 1), np.uint8)], axis=1)
    return (np.ascontiguousarray(c[:, e].reshape(128, -1)), np.ascontiguousarray(s[:, e]))
def join(*qs):
    return (np.concatenate([q[0] for q in qs], axis=1), np.concatenate([q[1] for q in qs], axis=1))
def put(q, e, v):
    c, s = q[0].reshape(128, -1, 4).copy(), q[1].copy(); c[:, e] = v[0].reshape(128, -1, 4); s[:, e] = v[1]
    return (c.reshape(128, -1), s)
def pk(c, s):
    return (np.ascontiguousarray(c), mx_ref.live(s))
def emit(q):
    return q[0], q[1]
def packed(v, rng):
    q = [mx_ref.quantize(np.ascontiguousarray(v[r])) for r in range(N)]
    return np.stack([a for a, b in q]), np.stack([mx_ref.plane(b, rng) for a, b in q])
def values_of_codes():
    e, c = np.zeros((128, 128, 4), np.float32), np.zeros((128, 2, 4), np.uint8)
    e[np.arange(128), np.arange(128), 0] = 1
    c[:127, :, 0] = np.arange(256).reshape(2, 128).T[:127]
    return mx_ref.matmul(mx_ref.quantize(e.reshape(128, 512).astype(BF)), (c.reshape(128, 8), np.full((16, 2), 127, np.uint8))).T.reshape(-1).astype(np.float64)
CODE_VALUE, SCALE_VALUE = values_of_codes(), 2.0 ** (np.arange(256) - 127.0)
def decode(q):
    return (CODE_VALUE[q[0]].reshape(16, 8, -1, 4) * SCALE_VALUE[q[1]][:, None, :, None] + 0.0).reshape(128, -1).astype(np.float32)
def f(rng, *shape):
    return mx_ref.flush((rng.standard_normal(shape, dtype=np.float32) * np.exp2(rng.integers(-2, 3, shape[:-1] + (1,)))).astype(BF))
def wide(rng, *shape, cols=0):
    v = rng.standard_normal(shape, dtype=np.float32) * np.exp2(rng.integers(-12, 13, shape)).astype(np.float32)
    if cols: v *= np.repeat(np.exp2(rng.integers(-cols, cols + 1, shape[:-2] + (1, shape[-1] // 4))) * (rng.random(shape[:-2] + (1, shape[-1] // 4)) > 0.0625), 4, axis=-1).astype(np.float32)
    return mx_ref.flush(v.astype(BF))
C, HALF = 448, 224
STEP = [1, 2, 3]
def numbers_of(rng):
    return {"x": np.array(f(rng, N, 128, 4 * C)), "lv": np.array(f(rng, N, 128, 4 * C)), "u": np.array(f(rng, N, 128, 512)), "v": np.array(f(rng, N, 128, 512))}
def names(rng):
    return rng.permuted(np.tile(np.arange(2 * C), (N, 8, 1)), axis=2)
def paired(rng, roots):
    p, n = np.flatnonzero(roots), np.flatnonzero(~roots)
    k = np.zeros(2 * C, np.int64)
    k[p] = rng.permutation(n)
    k[np.concatenate([n, np.arange(C, 2 * C)])] = rng.permutation(np.concatenate([p, np.arange(C, 2 * C)]))
    return k
def stored(k):
    return {"lt": np.stack([gtable(k[r][:, :C]) for r in range(N)]), "rt": np.stack([gtable(k[r][:, C:]) for r in range(N)])}
def layers(rng):
    return np.array(f(rng, N, 128, 2048)).reshape(N, 8, 16, 4, 8, 16, 4)
def weights(rng, w):
    c, p = packed(np.ascontiguousarray(w).reshape(N, 128, 2048), rng)
    return {"wc": c, "ws": p}
def setup_inputs(rng):
    return {**numbers_of(rng), **stored(names(rng)), **weights(rng, layers(rng))}
def setup_inputs_ties(rng):
    d = numbers_of(rng)
    o = rng.permutation(N)
    k = rng.integers(-1, 2, (N, 8, 4, C)).astype(np.float32)
    k[o[1]] = 1
    e = names(rng)
    for g in range(8):
        p = rng.permutation(C) < HALF
        k[o[3], g, 0] = np.where(p, 1.0, -1.0)
        if g % 2:
            k[o[3], g, 1] = np.minimum(k[o[3], g, 1], 0)
            k[o[3], g, 2] = k[o[3], g, 0]
        e[o[3], g] = paired(rng, p)
    x = d["x"].reshape(N, 8, 16, C, 4)
    x[:, :, :8] = 0
    x[:, :, :4, :, 0] = k.astype(BF)
    c = np.ones(N, np.float32)
    c[o[0]] = 0
    c[o[2]] = -1
    u = d["u"].reshape(N, 128, 128, 4)
    for g in range(8):
        for h in range(16 * g, 16 * g + 4):
            u[:, :, h] = 0
            u[:, h, h, 0] = c.astype(BF)
    w = layers(rng)
    w[:, :, :, :, :, :8] = 0
    return {"x": x.reshape(N, 128, 4 * C), "lv": d["lv"], "u": u.reshape(N, 128, 512), "v": d["v"], **stored(e), **weights(rng, w)}
def setup_inputs_near(rng):
    d = numbers_of(rng)
    o = rng.permutation(N)
    t = int(np.flatnonzero(o == 0)[0])
    k = np.where(o % 2 == 0, 2.0 ** -30, 1.0).astype(np.float32)
    x = d["x"].astype(np.float32).reshape(N, 8, 16, C, 4)
    lv = d["lv"].astype(np.float32).reshape(N, 8, 16, C, 4)
    s = rng.integers(-1, 2, (N, 8, 4, C)) * np.where(o % 2 == 0, 2.0 ** -28, 1.0)[:, None, None, None]
    x[:, :, :8] = 0
    x[:, :, :4, :, 0] = 1.125 * s
    x[:, :, 4:8, :, 0] = -1.25 * s
    for r in range(N):
        at = [0, C - 1, int(rng.integers(C)), int(rng.integers(C))]
        for g, j in zip(rng.permutation(8)[:4], at): x[r, g, rng.integers(4), j, 0] = 2.0 ** 30 * rng.choice([-1.0, 1.0])
    x[t] = 0
    x[t, :, 7, :, 3] = 2.0 ** -29
    for z in (x, lv):
        z[:, :, 15, :, 3] = 4.0
        z[t, :, 8:] = rng.choice([-1.0, 1.0], (8, 8, C, 4)) * 2.0 ** -26
        z[t, :, 8:12, :, 0] *= np.float32(2.0 ** -4)
        z[t, ::2, 9:12:2, :, 0] = 2.0 ** -30
        z[t, :, 15, :, 3] = 2.0 ** -28
    u = d["u"].reshape(N, 128, 128, 4)
    w = layers(rng)
    w[:, :, :8] = 0
    w[:, :, :, :, :, :8] = 0
    w[:, :, :, 3, :, 15] = 0
    w[:, :, 15, 3, :, 15, 3] = 4.0
    w[t, :, 15, 3, :, 7, 3] = 4.0
    for g in range(8):
        for i in range(4):
            h = 16 * g + i
            u[:, :, h] = 0
            u[:, h, h, 0] = (1.125 * k).astype(BF)
            u[:, h + 4, h, 0] = k.astype(BF)
            u[t, :, h] = 0
            u[t, h, h, 1] = 1.125 * 2.0 ** -30
            u[t, h + 4, h, 1] = 2.0 ** -30
            w[t, g, 8 + i, 1, g, i, 0] = 1.125 * 2.0 ** -5
            w[t, g, 8 + i, 1, g, i + 4, 0] = -1.25 * 2.0 ** -5
    return {"x": x.reshape(N, 128, 4 * C).astype(BF), "lv": lv.reshape(N, 128, 4 * C).astype(BF), "u": u.reshape(N, 128, 512), "v": d["v"], **stored(names(rng)), **weights(rng, w)}
def setup_inputs_odd(rng):
    d = numbers_of(rng)
    x = np.zeros((N, 8, 16, C, 4), np.float32)
    lv = np.zeros((N, 8, 16, C, 4), np.float32)
    a = np.exp2(rng.integers(5, 9, (8, 1)).astype(np.float32))
    b = rng.integers(0, 2, (N, 8, 4, C))
    x[:, :, 0, :, 3] = 1.96875 * 2.0 ** 8
    x[:, :, 0:8:2, :, 0] = (8 + b) * 2.0 ** -8
    x[:, :, 1:8:2, :, 0] = (9 - b) * 2.0 ** -8
    for t in (x, lv):
        t[:, :, 7, :, 1] = 1.125 * a
        t[:, :, 7, :, 2] = 0.0703125 * a
    x[:, :, 9, :, 0] = -a
    u = d["u"].reshape(N, 128, 128, 4)
    w = np.zeros((N, 8, 16, 4, 8, 16, 4), np.float32)
    for g in range(8):
        w[:, g, 7, 0, g, 9, 1] = 28.0
        for i in range(4):
            u[:, :, 16 * g + i] = 0
            u[:, 16 * g + 2 * i, 16 * g + i, 0] = 1.0
            u[:, 16 * g + 2 * i + 1, 16 * g + i, 0] = -1.0
            w[:, g, 7, i, g, 10, 2] = [1.0, 1.25, 0.75, 0.5625][i] * 2.0 ** -5
    return {"x": x.reshape(N, 128, 4 * C).astype(BF), "lv": lv.reshape(N, 128, 4 * C).astype(BF), "u": u.reshape(N, 128, 512), "v": d["v"], **stored(names(rng)), **weights(rng, w.astype(BF))}
def setup_inputs_ends(rng):
    d = numbers_of(rng)
    n = np.arange(N)
    o = np.array([1, 0, 2, 3])[(n & 3) ^ rng.integers(0, 4, 2)[n >> 2]]
    x = np.zeros((N, 8, 16, C, 4), np.float32)
    lv = np.zeros((N, 8, 16, C, 4), np.float32)
    a = np.zeros((N, 8, 4))
    k = names(rng)
    w = np.zeros((N, 128, 4, 128, 4), np.float32)
    i, c = np.arange(128), np.arange(C)
    for r in range(N):
        a[r] = rng.choice([-1.0, 1.0], (8, 4)) * (rng.permutation(8) > 1)[:, None]
        roots = rng.permutation(C) < HALF
        s = rng.choice([-1.0, 1.0], (2, 8, 16, C, 4))
        size = (0.6 + 0.05 * rng.random((2, 8, 16, C, 4))) * 2.0 ** 30
        if o[r] == 0:
            s[:] = -1.0
            k[r] = np.concatenate([2 * C - 1 - c, C - 1 - c])
        if o[r] == 1:
            s[0] = np.where(roots, 1.0, -1.0)[None, None, :, None]
            for g in range(8): k[r, g] = paired(rng, ~roots if a[r, g, 0] < 0 else roots)
        if o[r] == 2: k[r] = np.concatenate([(c + 1) % C, 2 * C - 1 - c])
        if o[r] == 3:
            s[0] = s[0][:, :1, :, :1]
            size[:] = 2.0 ** -28
            for j, g in enumerate(rng.permutation(8)):
                k[r, g] = np.concatenate([rng.permutation(C) + C * (j % 2), rng.permutation(C) + C * (1 - j % 2)])
        x[r], lv[r] = s * size
        if o[r] == 2: w[r] = rng.choice([-1.0, 1.0], (128, 4, 128, 4)) * 2.0 ** -6
        else:
            for b in range(4): w[r, i, b, i, b] = -1.0 if o[r] < 2 else 64.0
    size = np.where(o == 3, 2.0 ** -30, 2.0 ** 30)
    u = d["u"].reshape(N, 128, 128, 4)
    for j in range(4): u[:, :, j::16] = (a[:, :, j] * size[:, None] + 0.0).astype(np.float32).astype(BF)[:, None, :, None]
    v = rng.choice([-1.0, 1.0], (N, 128, 512)) * size[:, None, None]
    return {"x": x.reshape(N, 128, 4 * C).astype(BF), "lv": lv.reshape(N, 128, 4 * C).astype(BF), "u": u.reshape(N, 128, 512), "v": v.astype(np.float32).astype(BF), **stored(k), **weights(rng, w.astype(BF))}
def setup_inputs_spread(rng):
    d = setup_inputs(rng)
    d["x"] = wide(rng, N, 128, 4 * C, cols=6)
    d["lv"] = wide(rng, N, 128, 4 * C, cols=6)
    return d
def check_inputs(d):
    b = []
    for k in ("x", "lv", "u", "v"):
        a = np.abs(d[k].astype(np.float32))
        if not (np.isfinite(a).all() and ((a == 0) | (a >= 2.0 ** -30) & (a <= 2.0 ** 30)).all()): b.append("a value of " + k)
    none, least, most = [emit(mx_ref.quantize(np.full((128, 16), k, np.float32).astype(BF)))[1][0, 0] for k in (0.0, 2.0 ** -6, 2.0 ** 6)]
    for r in range(N):
        if (np.sort(np.concatenate([gentries(d["lt"][r]), gentries(d["rt"][r])], axis=1), axis=1) != np.arange(2 * C)).any(): b.append("lt and rt: not every name once in a group")
        if ((d["wc"][r] == 0x7F) | (d["wc"][r] == 0xFF)).any(): b.append("wc: a code that is no number")
        s = mx_ref.live(d["ws"][r])
        if ((s != none) & ((s < least) | (s > most))).any(): b.append("ws: a scale out of range")
        if (((d["wc"][r].reshape(16, 8, 512, 4) & 0x7F) != 0) & (s == none)[:, None, :, None]).any(): b.append("wc: a code other than zero under the scale of zeros")
    return b
def rewrite(left, right, act, turn):
    g, c = np.nonzero((left < C) & (act > 0) & (np.take_along_axis(act, left % C, 1) < 0))
    s = left[g, c]
    a, b, z = left[g, s], right[g, s], right[g, c]
    t = turn[g, a % C] > 0
    left, right = left.copy(), right.copy()
    left[g, c], right[g, c] = np.where(t, a, s), np.where(t, s, b)
    left[g, s], right[g, s] = np.where(t, b, a), z
    return left, right
def reference(x, lv, u, v, lt, rt, wc, ws):
    qu = [mx_ref.quantize(u[r]) for r in range(N)]
    lay = [pk(wc[r], ws[r]) for r in range(N)]
    left, right = [gentries(lt[r]) for r in range(N)], [gentries(rt[r]) for r in range(N)]
    now, leaf = [x[r] for r in range(N)], [lv[r] for r in range(N)]
    for step in STEP:
        made = []
        for r in range(N):
            s = mx_ref.matmul(qu[r], mx_ref.quantize(now[r])).reshape(8, 16, C)
            for j in range(2): left[r], right[r] = rewrite(left[r], right[r], s[:, 2 * j], s[:, 2 * j + 1])
            win = np.concatenate([now[r], leaf[r]], axis=1)
            z = mx_ref.quantize(((gcols(win, left[r]).astype(np.float32) + gcols(win, right[r]).astype(np.float32)) * np.float32(0.5)).astype(BF))
            made.append(tile([mx_ref.matmul(pick(lay[r], np.arange(128 * b, 128 * b + 128)), z) * np.float32(0.03125) for b in range(4)]))
        for r in range(N):
            p = r ^ step
            m = np.take_along_axis(left[p], right[r] % C, 1) % C
            far = gcols(decode(mx_ref.quantize(made[p])).astype(BF), m[:, :HALF])
            leaf[r] = np.concatenate([far, gcols(made[r], m[:, HALF:])], axis=1)
            now[r] = (now[r].astype(np.float32) + leaf[r].astype(np.float32)).astype(BF)
    y, gr = np.zeros((N, 128, C), np.float32), np.zeros((N, 8, 2 * C), np.float32)
    oc, osc = np.zeros((N, 128, 4 * C), np.uint8), np.zeros((N, 16, C), np.uint8)
    for r in range(N):
        q = mx_ref.quantize(now[r])
        y[r] = mx_ref.matmul(mx_ref.quantize(v[r]), q)
        gr[r] = np.concatenate([left[r], right[r]], axis=1)
        oc[r], osc[r] = emit(q)
    return {"y": y, "gr": gr, "oc": oc, "osc": osc}

@@ -1,0 +1,428 @@
+from concourse.mybir import dt, AluOpType, ActivationFunctionType
+
+ROUNDS = [1, 2, 3]
+PARTS = [(0, 256), (256, 448)]
+ADD, SUB, MUL = AluOpType.add, AluOpType.subtract, AluOpType.mult
+GE, GT, LT = AluOpType.is_ge, AluOpType.is_gt, AluOpType.is_lt
+NE, ANDB, SHR = AluOpType.not_equal, AluOpType.bitwise_and, AluOpType.arith_shift_right
+COPY, RELU, SIGN, MAX = ActivationFunctionType.Copy, ActivationFunctionType.Relu, ActivationFunctionType.Sign, AluOpType.max
+F32, BF, I32, U16, U8, MXC = "float32", "bfloat16", "int32", "uint16", "uint8", "float8_e4m3fn_x4"
+
+
+def _sb(n, d):
+    return ("sbuf", [128, n], d)
+
+
+SCRATCH = {
+    "xa": _sb(1792, BF), "xb": _sb(1792, BF), "lvt": _sb(1792, BF), "ut": _sb(512, BF), "vt": _sb(512, BF),
+    "one": _sb(512, BF), "et": _sb(2048, BF), "win": _sb(4 * 896, BF), "zr": _sb(1792, BF), "zt": _sb(1792, BF),
+    "hw": _sb(1792, BF), "sh": _sb(896, BF), "yb": _sb(448, F32),
+    "qu": _sb(128, MXC), "su": _sb(128, U8), "qk": _sb(128, MXC), "sk": _sb(128, U8), "qv": _sb(128, MXC), "sv": _sb(128, U8),
+    "qe": _sb(512, MXC), "se": _sb(512, U8), "qw": _sb(512, MXC), "sw": _sb(512, U8), "qx": _sb(448, MXC), "sx": _sb(448, U8),
+    "qz": _sb(448, MXC), "sz": _sb(448, U8),
+    "lti": _sb(28, I32), "rti": _sb(28, I32), "pi": _sb(1, I32), "ci": _sb(28, I32), "ui": _sb(8, I32), "ki": _sb(7, I32),
+    "kf": _sb(7, F32), "kt": _sb(16, F32), "cl2": _sb(4, U16), "cl1": _sb(2, U16), "clu": _sb(8, U16),
+    "tb0": _sb(992, F32), "tt": _sb(1888, F32), "k1": _sb(4, F32), "k2": _sb(4, F32), "tg": _sb(1792, BF), "tg2": _sb(448, BF), "ta": _sb(448, F32), "tp": _sb(448, F32),
+    "tm": _sb(448, F32), "ls": _sb(896, F32), "wq": _sb(896, F32), "sg": _sb(912, BF), "gg1": _sb(896, BF), "gg2": _sb(448, BF),
+    "gg3": _sb(448, BF), "h1": _sb(896, F32), "h2": _sb(448, BF), "p0": _sb(896, F32), "p1": _sb(896, F32), "a1": _sb(448, F32),
+    "ms": _sb(448, F32), "xx": _sb(96, F32), "cw1": _sb(96, F32), "xy": _sb(64, F32),
+    "nl": _sb(64, U16), "nl1": _sb(64, U16), "nf": _sb(64, F32), "pw": _sb(32, U16),
+    "t28": _sb(28, F32), "ff": _sb(112, F32), "pr": _sb(112, F32), "p3": _sb(28, F32), "uu": _sb(56, F32),
+    "dl0": _sb(112, F32), "dl1": _sb(112, F32), "d30": _sb(28, F32), "d31": _sb(28, F32),
+    "ps": ("psum", [128, 4096], F32),
+}
+for _k in range(3):
+    SCRATCH.update({"rc%d" % _k: _sb(64, U16), "mu%d" % _k: _sb(32, U16), "lr%d" % _k: _sb(28, U16), "lm%d" % _k: _sb(14, U16),
+                    "qs%d" % _k: _sb(224, MXC), "ss%d" % _k: _sb(224, U8), "ql%d" % _k: _sb(224, MXC), "sl%d" % _k: _sb(224, U8)})
+ENG_SEM = {"v": "eV", "s": "eS", "t": "eT", "p": "eP"}
+SEMAPHORES = list(ENG_SEM.values()) + ["loc"] + ["d%d" % i for i in range(32)] + ["%s%d" % (a, k) for a in ("aR", "aM", "aC", "aS") for k in range(3)]
+
+
+def rank_program(g, core, T, topo):
+    rank = T.rank_of(core)
+    if rank is None:
+        return
+    eng = {"v": g.vector, "s": g.scalar, "t": g.tensor, "p": g, "y": g.sync}
+    cnt = {"v": 0, "s": 0, "t": 0, "p": 0}
+    know = {q: {} for q in eng}
+    snap, recs, ndma, nloc = {}, {}, [0], [0]
+
+    def wait(q, sem, val):
+        if know[q].get(sem, 0) >= val:
+            return
+        eng[q].wait_ge(T.sem[sem], val)
+        for s, n in snap.get((sem, val), {}).items():
+            know[q][s] = max(know[q].get(s, 0), n)
+        know[q][sem] = max(know[q].get(sem, 0), val)
+
+    def need(q, src, reads, writes):
+        w = {}
+        for acc, wr in [(a, False) for a in reads] + [(a, True) for a in writes]:
+            name, cols = acc
+            for rn, rcols, rwr, rsrc, sem, val in recs.get(name, []):
+                if name == "ps":
+                    if rsrc == src or not (cols & rcols):
+                        continue
+                elif not (wr or rwr) or not (cols & rcols):
+                    continue
+                elif rsrc == src and not rwr:
+                    continue
+                w[sem] = max(w.get(sem, 0), val)
+        for sem in sorted(w):
+            wait(q, sem, w[sem])
+
+    def note(src, sem, val, reads, writes):
+        for name, cols in writes:
+            recs[name] = [r for r in recs.get(name, []) if not (r[1] <= cols)]
+        for name, cols in reads:
+            recs[name] = [r for r in recs.get(name, []) if not (not r[2] and r[3] == src and src != "dma" and r[1] <= cols)]
+        for acc, wr in [(a, False) for a in reads] + [(a, True) for a in writes]:
+            recs.setdefault(acc[0], []).append((acc[0], acc[1], wr, src, sem, val))
+
+    def acc(*views):
+        out = []
+        for v in views:
+            for name, cols in v[1]:
+                if name == "ps":
+                    cols = frozenset(x // 512 for x in cols)
+                out.append((name, frozenset(cols)))
+        return out
+
+    def V(name, a, b, s=1):
+        return (T[name][:, a:b] if s == 1 else T[name][:, a:b:s], [(name, range(a, b, s))])
+
+    def I(name, a, b, off, c, d):
+        return (T[name][:, a:b].indirect(T[off][:, c:d]), [(name, range(a, b)), (off, range(c, d))])
+
+    def do(q, call, out, *ins):
+        outs = list(out) if isinstance(out, list) else [out]
+        reads, writes = [], acc(*[(o[0], o[1][:1]) for o in outs])
+        for o in outs:
+            reads += acc((None, o[1][1:]))
+        reads += acc(*ins)
+        need(q, q, reads, writes)
+        r = call(eng[q])
+        cnt[q] += 1
+        sem = ENG_SEM[q]
+        r.then_inc(T.sem[sem], 1)
+        k = dict(know[q])
+        k[sem] = cnt[q]
+        snap[(sem, cnt[q])] = k
+        note(q, sem, cnt[q], reads, writes)
+
+    def dma(q, out_ap, in_ap, reads=(), writes=()):
+        need(q, "dma", acc((None, reads)), acc((None, writes)))
+        sem = "d%d" % ndma[0]
+        ndma[0] += 1
+        eng[q].dma_start(out_ap, in_ap).then_inc(T.sem[sem], 16)
+        snap[(sem, 16)] = dict(know[q])
+        note("dma", sem, 16, acc((None, reads)), acc((None, writes)))
+
+    def send(dst, out_ap, in_ap, sem, view):
+        need("p", "rem", acc(view), [])
+        a = topo.addr(dst)
+        g.remote_dma(out_ap, in_ap, T.sem[sem], T.sem["loc"], a[1], a[0], topo.mask(core, dst))
+        nloc[0] += len(topo.engines(core, dst))
+
+    def lands(name, n, sem, src):
+        recs.setdefault(name, []).append((name, frozenset(range(n)), True, "rem", sem, len(topo.engines(src, core))))
+
+    def tt(out, a, b, op):
+        do("v", lambda e: e.tensor_tensor(out[0], a[0], b[0], op), out, a, b)
+
+    def ts(out, a, s1, s2, op0, *op1):
+        sc = [x for x in (s1, s2) if isinstance(x, tuple)]
+        do("v", lambda e: e.tensor_scalar(out[0], a[0], s1[0] if isinstance(s1, tuple) else s1, s2[0] if isinstance(s2, tuple) else s2, op0, *op1), out, a, *sc)
+
+    def cp(out, a):
+        do("v", lambda e: e.tensor_copy(out[0], a[0]), out, a)
+
+    def tr(out, a):
+        do("v", lambda e: e.transpose(out[0], a[0]), out, a)
+
+    def fill(out, c):
+        do("v", lambda e: e.memset(out[0], c), out)
+
+    def act(out, a, func=COPY, scale=1.0):
+        if isinstance(scale, tuple):
+            do("s", lambda e: e.activation(out[0], a[0], func, scale=scale[0]), out, a, scale)
+        else:
+            do("s", lambda e: e.activation(out[0], a[0], func, scale=scale), out, a)
+
+    def quant(q, s, a, b, tile, ta, tb):
+        do("v", lambda e: e.quantize_mx(T[q][:, a:b], T[s][:, a:b], T[tile][:, ta:tb]), [V(q, a, b), V(s, a, b)], V(tile, ta, tb))
+
+    def mm(bank, n, ql, sl, la, qr, sr, a, b):
+        o = V("ps", 512 * bank, 512 * bank + n)
+        do("t", lambda e: e.matmul_mx(o[0], T[ql][:, la:la + 128], T[sl][:, la:la + 128], T[qr][:, a:b], T[sr][:, a:b], True, True), o,
+           V(ql, la, la + 128), V(sl, la, la + 128), V(qr, a, b), V(sr, a, b))
+
+    def PS(bank, n):
+        return V("ps", 512 * bank, 512 * bank + n)
+
+    def conv2(buf, o, out):
+        tr(V("xx", 16, 80), V(buf, o + 5, o + 510, 8))
+        tr(V(buf, o + 896, o + 992), V("xx", 0, 96))
+        cp(out, I(buf, o, o + 992, "cl2", 0, 4))
+
+    def conv1(out):
+        tr(V("xy", 16, 48), V("cw1", 0, 32))
+        tr(V("cw1", 32, 96), V("xy", 0, 64))
+        cp(out, I("cw1", 0, 96, "cl1", 0, 2))
+
+    def rewrite(plus, minus, acting, turns, base, nxt, dl, d3):
+        tt(V("ff", 1, 112, 2), plus, minus, acting)
+        for o, i, a in turns:
+            tt(o, i, a, MUL)
+        tt(V("pr", 0, 112), V("ff", 0, 112), V(dl, 0, 112), MUL)
+        tt(V("p3", 0, 28), V("ff", 0, 56, 2), V(d3, 0, 28), MUL)
+        tt(V("uu", 0, 56), V("pr", 0, 56), V("pr", 56, 112), ADD)
+        tt(V("uu", 1, 56, 2), V("uu", 1, 56, 2), V("p3", 0, 28), ADD)
+        tt(nxt, base, V("uu", 0, 56), ADD)
+
+    L0, R0, LR0 = V("tb0", 5, 448, 16), V("tb0", 13, 448, 16), V("tb0", 5, 448, 8)
+    L1, R1, LR1 = V("tt", 901, 1344, 16), V("tt", 909, 1344, 16), V("tt", 901, 1344, 8)
+
+    def ahead_lists():
+        tr(V("tp", 0, 448), V("p0", 0, 448))
+        ts(V("cw1", 0, 28), V("tp", 4, 448, 16), 896.0, None, ADD)
+        conv1(V("pw", 0, 32))
+        tt(V("dl0", 56, 112, 2), R0, L0, SUB)
+        tt(V("dl0", 57, 112, 2), V("tp", 13, 448, 16), R0, SUB)
+
+    def ahead_children():
+        tr(V("ta", 0, 448), V("a1", 0, 448))
+        tt(V("dl0", 0, 56), V("ta", 5, 448, 8), LR0, SUB)
+        tt(V("d30", 0, 28), L0, V("ta", 13, 448, 16), SUB)
+
+    def scores(half):
+        a = 224 * half
+        mm(4 + half, 224, "qk", "sk", 0, "qx", "sx", a, a + 224)
+
+    def signs(half):
+        a = 224 * half
+        act(V("sg", a, a + 224), PS(4 + half, 224), SIGN)
+        act(V("sg", 448 + a, 672 + a), PS(4 + half, 224), SIGN, V("kf", 5, 6))
+
+    def local_signs(half):
+        a = 224 * half
+        tr(V("tg", 896 + a, 1120 + a), V("sg", a, a + 224))
+
+    dma("y", T.lti[:, 0:28], T.lt[:, :], writes=[("lti", range(28))])
+    dma("s", T.rti[:, 0:28], T.rt[:, :], writes=[("rti", range(28))])
+    dma("s", T.ut[:, :], T.u[:, :], writes=[("ut", range(512))])
+    for h in range(2):
+        dma("y", T.xa[:, 896 * h:896 * h + 896], T.x[:, 896 * h:896 * h + 896], writes=[("xa", range(896 * h, 896 * h + 896))])
+    dma("s", T.lvt[:, :], T.lv[:, :], writes=[("lvt", range(1792))])
+    dma("y", T.qw[:, 0:512].bitcast(dt.uint8), T.wc[:, :], writes=[("qw", range(512))])
+    dma("y", T.sw[:, 0:512], T.ws[:, :], writes=[("sw", range(512))])
+    dma("y", T.vt[:, :], T.v[:, :], writes=[("vt", range(512))])
+    for k in range(3):
+        p = T.cores[rank ^ ROUNDS[k]]
+        lands("lr%d" % k, 28, "aR%d" % k, p)
+        lands("lm%d" % k, 14, "aM%d" % k, p)
+        lands("ql%d" % k, 224, "aC%d" % k, p)
+        lands("sl%d" % k, 224, "aS%d" % k, p)
+    do("p", lambda e: e.iota(T.pi[:, 0:1], [[0, 1]], 0, 1), V("pi", 0, 1))
+    do("p", lambda e: e.iota(T.ci[:, 0:28], [[32, 14], [0, 2]], -896, 0), V("ci", 0, 28))
+    do("p", lambda e: e.iota(T.ui[:, 0:8], [[16, 8]], 0, 0), V("ui", 0, 8))
+    do("p", lambda e: e.iota(T.k1[:, 0:4], [[7, 2], [224, 2]], 0, 0, allow_small_or_imprecise_dtypes=True), V("k1", 0, 4))
+    do("p", lambda e: e.iota(T.k2[:, 0:4], [[8, 2], [256, 2]], 5, 0, allow_small_or_imprecise_dtypes=True), V("k2", 0, 4))
+    fill(V("one", 0, 512), 1.0)
+    for b in range(4):
+        do("p", lambda e: e.affine_select(T.et[:, 512 * b:512 * b + 512], T.one[:, 0:512], [[-1, 512]], AluOpType.is_equal, 0.0, b, 4),
+           V("et", 512 * b, 512 * b + 512), V("one", 0, 512))
+    fill(V("tb0", 0, 448), 0.0)
+    act(V("tb0", 448, 896), V("tb0", 0, 448), COPY, 0.0)
+    for name, a, b in (("xx", 0, 96), ("cw1", 0, 32), ("xy", 0, 64), ("tt", 896, 1344), ("tt", 1344, 1792), ("sg", 896, 912),
+                       ("p0", 0, 448), ("gg1", 448, 896), ("h1", 448, 896), ("p1", 0, 448)):
+        act(V(name, a, b), V("tb0", 448, 448 + b - a), COPY, 0.0)
+    for i, (s1, s2, ops) in enumerate([(15, None, (ANDB,)), (4, 1, (SHR, ANDB)), (1, None, (ANDB,)), (31, None, (ANDB,)), (3, None, (ANDB,)), (4, None, (ANDB,))]):
+        ts(V("ki", i, i + 1), V("pi", 0, 1), s1, s2, *ops)
+    cp(V("kf", 0, 6), V("ki", 0, 6))
+
+    def K(i):
+        return V("kt", i, i + 1)
+    X_, H_, B_ = V("kf", 0, 1), V("kf", 1, 2), V("kf", 2, 3)
+    tt(K(0), B_, H_, SUB)
+    ts(K(2), H_, -32.0, 925.0, MUL, ADD)
+    ts(K(4), B_, 2.0, -860.0, MUL, ADD)
+    tt(K(1), K(0), K(0), MUL)
+    ts(K(3), B_, -4.0, K(2), MUL, ADD)
+    ts(K(5), K(1), -1.0, None, MUL)
+    tt(K(4), K(4), K(3), ADD)
+    ts(K(3), X_, -14.0, K(3), MUL, ADD)
+    tt(K(4), K(4), K(1), MUL)
+    tt(K(3), K(3), K(1), MUL)
+    tt(K(4), K(4), X_, ADD)
+    ts(K(3), X_, 16.0, K(3), MUL, ADD)
+    ts(V("k1", 0, 4), V("k1", 0, 4), K(5), K(3), MUL, ADD)
+    tt(V("k1", 0, 4), V("k1", 0, 4), V("k2", 0, 4), ADD)
+    cp(V("cl2", 0, 4), V("k1", 0, 4))
+    ts(V("clu", 0, 8), V("ui", 0, 8), V("kf", 4, 5), None, ADD)
+    for k in range(2):
+        ts(V("cl1", k, k + 1), K(4), 16.0 * k, None, ADD)
+    ts(V("kf", 6, 7), V("kf", 5, 6), 0.25, None, MUL)
+    ts(V("kf", 5, 6), V("kf", 5, 6), -0.25, 1.0, MUL, ADD)
+    ts(V("tb0", 4, 448, 16), V("ci", 0, 28), V("kf", 3, 4), None, ADD)
+    cp(L1, V("lti", 0, 28))
+    cp(R1, V("rti", 0, 28))
+    cp(V("nl", 0, 28), V("lti", 0, 28))
+    conv2("tt", 896, V("nf", 0, 64))
+    cp(L0, V("nf", 0, 28))
+    cp(R0, V("nf", 32, 60))
+    tr(V("ls", 0, 448), V("tb0", 0, 448))
+    act(V("ls", 448, 896), V("ls", 0, 448))
+    act(V("a1", 0, 448), I("ls", 0, 896, "nl", 0, 28))
+    quant("qu", "su", 0, 128, "ut", 0, 512)
+    do("v", lambda e: e.tensor_copy(T.qk[:, 0:128].bitcast(dt.uint32), T.qu[:, 0:128].bitcast(dt.uint32).indirect(T.clu[:, 0:8])),
+       V("qk", 0, 128), V("qu", 0, 128), V("clu", 0, 8))
+    do("s", lambda e: e.activation(T.sk[:, 0:128], T.su[:, 0:128].indirect(T.clu[:, 0:8]), COPY), V("sk", 0, 128), V("su", 0, 128), V("clu", 0, 8))
+    cp(I("p0", 0, 896, "nl", 0, 28), V("ls", 0, 448))
+    for h in range(2):
+        quant("qx", "sx", 224 * h, 224 * h + 224, "xa", 896 * h, 896 * h + 896)
+        scores(h)
+        if h == 0:
+            quant("qe", "se", 0, 512, "et", 0, 2048)
+    for h in range(2):
+        signs(h)
+    ahead_lists()
+    ahead_children()
+    for h in range(2):
+        local_signs(h)
+
+    xs, nl = ["xa", "xb"], "nl"
+    for k in range(3):
+        last = k == 2
+        p = T.cores[rank ^ ROUNDS[k]]
+        old, new = xs[k % 2], xs[(k + 1) % 2]
+        w = I("sg", 0, 896, nl, 0, 28)
+        do("s", lambda e: e.activation(T.gg1[:, 0:448], w[0], RELU, bias=T.kf[:, 6:7]), V("gg1", 0, 448), w, V("kf", 6, 7))
+        ts(V("gg3", 0, 448), I("sg", 0, 912, "pw", 0, 28), 0.75, -1.25, MUL, ADD)
+        act(V("gg2", 0, 448), I("gg1", 0, 896, nl, 0, 28))
+        tr(V("tg", 448, 896), V("gg1", 0, 448))
+        tr(V("tg", 1344, 1792), V("gg3", 0, 448))
+        tr(V("tg", 0, 448), V("gg2", 0, 448))
+        act(V("tt", 896, 1344), V("tg", 896, 1344), RELU)
+        act(V("tt", 902, 1344, 16), V("tg", 898, 1344, 16), RELU, -1.0)
+        if k == 0:
+            for b in range(4):
+                act(V("win", 896 * b, 896 * b + 448), V("xa", b, 1792, 4), COPY, 0.5)
+        else:
+            for b in range(4):
+                act(V("win", 896 * b, 896 * b + 224), V(old, b, 896, 4), COPY, 0.5)
+        rewrite(V("tg", 896, 1792, 16), V("tg", 452, 1344, 16), GT, [(V("ff", 0, 112, 2), V("ff", 1, 112, 2), V("tg", 1, 896, 16))],
+                LR0, LR1, "dl0", "d30")
+        tr(V("wq", 0, 448), V("tt", 896, 1344))
+        act(V("wq", 448, 896), V("wq", 0, 448), COPY, V("kf", 5, 6))
+        conv2("tt", 896, V("nl1", 0, 64))
+        act(V("h1", 0, 448), I("wq", 0, 896, "nl1", 0, 28))
+        act(V("h2", 0, 448), I("h1", 0, 896, "nl1", 0, 28))
+        cp(I("p1", 0, 896, "nl1", 0, 28), V("wq", 0, 448))
+        if k == 0:
+            for b in range(4):
+                act(V("win", 896 * b + 448, 896 * b + 896), V("lvt", b, 1792, 4), COPY, 0.5)
+        else:
+            for b in range(4):
+                act(V("win", 896 * b + 448, 896 * b + 672), PS(b, 224), COPY, 0.5)
+        if not last:
+            act(V("p0", 0, 448), V("wq", 0, 448), COPY, 0.0)
+        tt(V("dl1", 56, 112, 2), R1, L1, SUB)
+        tr(V("tt", 448, 896), V("h1", 0, 448))
+        tt(V("dl1", 0, 56), V("tt", 453, 896, 8), LR1, SUB)
+        tt(V("d31", 0, 28), L1, V("tt", 461, 896, 16), SUB)
+        tr(V("tg2", 0, 448), V("h2", 0, 448))
+        tr(V("tt", 1344, 1792), V("p1", 0, 448))
+        tt(V("dl1", 57, 112, 2), V("tt", 1357, 1792, 16), R1, SUB)
+        rewrite(V("tt", 898, 1792, 16), V("tt", 454, 1344, 16), MUL,
+                [(V("ff", 0, 56, 2), V("ff", 1, 56, 2), V("tg2", 3, 448, 16)), (V("ff", 56, 112, 2), V("ff", 57, 112, 2), V("tt", 451, 896, 16))],
+                LR1, LR0, "dl1", "d31")
+        nl = "rc%d" % k
+        conv2("tb0", 0, V(nl, 0, 64))
+        send(p, T["lr%d" % k][:, 0:28], T[nl][:, 32:60], "aR%d" % k, V(nl, 32, 60))
+        tr(V("ls", 0, 448), V("tb0", 0, 448))
+        for h, (c0, c1) in enumerate(PARTS):
+            for b in range(4):
+                act(V("zr", 448 * b + c0, 448 * b + c1), I("win", 896 * b, 896 * b + 896, nl, 32 + c0 // 16, 32 + c1 // 16))
+            if h == 0:
+                act(V("ls", 448, 896), V("ls", 0, 448))
+        for h, (c0, c1) in enumerate(PARTS):
+            for b in range(4):
+                o, w = V("zt", 4 * c0 + b, 4 * c1, 4), I("win", 896 * b, 896 * b + 896, nl, c0 // 16, c1 // 16)
+                tt(o, w, V("zr", 448 * b + c0, 448 * b + c1), ADD)
+            quant("qz", "sz", c0, c1, "zt", 4 * c0, 4 * c1)
+            for b in range(4):
+                mm(4 * h + b, c1 - c0, "qw", "sw", 128 * b, "qz", "sz", c0, c1)
+        if last:
+            for i, q in enumerate((5, 13)):
+                dma("y", T.gr[:, 448 * i:448 * i + 448], T.ls[q:128:16, 0:448], reads=[("ls", range(448))])
+        act(V("ms", 0, 448), I("ls", 0, 896, "lr%d" % k, 0, 28))
+        tr(V("tm", 0, 448), V("ms", 0, 448))
+        ts(V("t28", 0, 28), V("tm", 5, 448, 16), 448.0, -448.0, GE, MUL)
+        tt(V("cw1", 0, 28), V("tm", 5, 448, 16), V("t28", 0, 28), ADD)
+        mu, lm = "mu%d" % k, "lm%d" % k
+        conv1(V(mu, 0, 32))
+        send(p, T[lm][:, 0:14], T[mu][:, 14:28], "aM%d" % k, V(mu, 14, 28))
+        for h, (c0, c1) in enumerate(PARTS):
+            for b in range(4):
+                o, i = V("hw", 448 * b + c0, 448 * b + c1), PS(4 * h + b, c1 - c0)
+                if h == 0 or b % 2:
+                    act(o, i, COPY, 0.03125)
+                else:
+                    ts(o, i, 0.03125, None, MUL)
+        for b in range(4):
+            o, w = V("sh", b, 896, 4), I("hw", 448 * b, 448 * b + 448, mu, 0, 14)
+            if b % 2:
+                act(o, w)
+            else:
+                cp(o, w)
+        qs, ss, ql, sl = "qs%d" % k, "ss%d" % k, "ql%d" % k, "sl%d" % k
+        quant(qs, ss, 0, 224, "sh", 0, 896)
+        send(p, T[ql][:, 0:224].bitcast(dt.uint8), T[qs][:, 0:224].bitcast(dt.uint8), "aC%d" % k, V(qs, 0, 224))
+        send(p, T[sl][:, 0:224], T[ss][:, 0:224], "aS%d" % k, V(ss, 0, 224))
+        if not last:
+            cp(I("p0", 0, 896, nl, 0, 28), V("ls", 0, 448))
+            act(V("a1", 0, 448), I("ls", 0, 896, nl, 0, 28))
+        for b in range(4):
+            tt(V(new, 896 + b, 1792, 4), I("hw", 448 * b, 448 * b + 448, lm, 0, 14), V(old, 896 + b, 1792, 4), ADD)
+        quant("qx", "sx", 224, 448, new, 896, 1792)
+        if not last:
+            scores(1)
+            ahead_lists()
+            for b in range(4):
+                act(V("win", 896 * b + 672, 896 * b + 896), I("hw", 448 * b, 448 * b + 448, lm, 0, 14), COPY, 0.5)
+            for b in range(4):
+                act(V("win", 896 * b + 224, 896 * b + 448), V(new, 896 + b, 1792, 4), COPY, 0.5)
+            signs(1)
+            local_signs(1)
+            act(V("p1", 0, 448), V("ls", 0, 448), COPY, 0.0)
+        else:
+            quant("qv", "sv", 0, 128, "vt", 0, 512)
+            finish(mm, act, dma, V, PS, T, 1)
+        for b in range(4):
+            mm(b, 224, "qe", "se", 128 * b, ql, sl, 0, 224)
+        for b in range(4):
+            tt(V(new, b, 896, 4), V(old, b, 896, 4), PS(b, 224), ADD)
+        quant("qx", "sx", 0, 224, new, 0, 896)
+        if not last:
+            scores(0)
+            signs(0)
+            ahead_children()
+            local_signs(0)
+        else:
+            finish(mm, act, dma, V, PS, T, 0)
+    for q in "vstp":
+        wait("y", ENG_SEM[q], cnt[q])
+    for i in range(ndma[0]):
+        wait("y", "d%d" % i, 16)
+    g.wait_ge(T.sem["loc"], nloc[0])
+
+
+def finish(mm, act, dma, V, PS, T, half):
+    a, b = 224 * half, 224 * half + 224
+    mm(4 + half, 224, "qv", "sv", 0, "qx", "sx", a, b)
+    dma("y", T.oc[:, 4 * a:4 * b], T.qx[:, a:b].bitcast(dt.uint8), reads=[("qx", range(a, b))])
+    for k in range(4):
+        dma("y", T.osc[4 * k:4 * k + 4, a:b], T.sx[32 * k:32 * k + 4, a:b], reads=[("sx", range(a, b))])
+    act(V("yb", a, b), PS(4 + half, 224))
+    dma("s", T.y[:, a:b], T.yb[:, a:b], reads=[("yb", range(a, b))])

@@ -3,10 +3,16 @@ from concourse.mybir import dt, AluOpType, ActivationFunctionType
 ROUNDS = [1, 2, 3]
 PARTS = [(0, 256), (256, 448)]
 ADD, SUB, MUL = AluOpType.add, AluOpType.subtract, AluOpType.mult
-GE, GT, LT = AluOpType.is_ge, AluOpType.is_gt, AluOpType.is_lt
-NE, ANDB, SHR = AluOpType.not_equal, AluOpType.bitwise_and, AluOpType.arith_shift_right
-COPY, RELU, SIGN, MAX = ActivationFunctionType.Copy, ActivationFunctionType.Relu, ActivationFunctionType.Sign, AluOpType.max
+GE, GT, MAX = AluOpType.is_ge, AluOpType.is_gt, AluOpType.max
+ANDB, SHR = AluOpType.bitwise_and, AluOpType.arith_shift_right
+COPY, RELU, SIGN = ActivationFunctionType.Copy, ActivationFunctionType.Relu, ActivationFunctionType.Sign
 F32, BF, I32, U16, U8, MXC = "float32", "bfloat16", "int32", "uint16", "uint8", "float8_e4m3fn_x4"
+EPS = 2.0 ** -93
+WIN, MID = 4096, 2048
+NODE = MID - 224
+NONE = 240
+SW = 1536
+TW = SW + 96
 
 
 def _sb(n, d):
@@ -15,20 +21,22 @@ def _sb(n, d):
 
 SCRATCH = {
     "xa": _sb(1792, BF), "xb": _sb(1792, BF), "lvt": _sb(1792, BF), "ut": _sb(512, BF), "vt": _sb(512, BF),
-    "one": _sb(512, BF), "et": _sb(2048, BF), "win": _sb(4 * 896, BF), "zr": _sb(1792, BF), "zt": _sb(1792, BF),
+    "one": _sb(512, BF), "et": _sb(2048, BF), "win": _sb(4 * WIN, BF), "zr": _sb(1792, BF), "zt": _sb(1792, BF),
     "hw": _sb(1792, BF), "sh": _sb(896, BF), "yb": _sb(448, F32),
-    "qu": _sb(128, MXC), "su": _sb(128, U8), "qk": _sb(128, MXC), "sk": _sb(128, U8), "qv": _sb(128, MXC), "sv": _sb(128, U8),
+    "qu": _sb(128, MXC), "su": _sb(128, U8), "qa": _sb(128, MXC), "sa": _sb(128, U8), "qb": _sb(128, MXC), "sb": _sb(128, U8),
+    "qv": _sb(128, MXC), "sv": _sb(128, U8),
     "qe": _sb(512, MXC), "se": _sb(512, U8), "qw": _sb(512, MXC), "sw": _sb(512, U8), "qx": _sb(448, MXC), "sx": _sb(448, U8),
     "qz": _sb(448, MXC), "sz": _sb(448, U8),
-    "lti": _sb(28, I32), "rti": _sb(28, I32), "pi": _sb(1, I32), "ci": _sb(28, I32), "ui": _sb(8, I32), "ki": _sb(7, I32),
-    "kf": _sb(7, F32), "kt": _sb(16, F32), "cl2": _sb(4, U16), "cl1": _sb(2, U16), "clu": _sb(8, U16),
-    "tb0": _sb(992, F32), "tt": _sb(1888, F32), "k1": _sb(4, F32), "k2": _sb(4, F32), "tg": _sb(1792, BF), "tg2": _sb(448, BF), "ta": _sb(448, F32), "tp": _sb(448, F32),
-    "tm": _sb(448, F32), "ls": _sb(896, F32), "wq": _sb(896, F32), "sg": _sb(912, BF), "gg1": _sb(896, BF), "gg2": _sb(448, BF),
-    "gg3": _sb(448, BF), "h1": _sb(896, F32), "h2": _sb(448, BF), "p0": _sb(896, F32), "p1": _sb(896, F32), "a1": _sb(448, F32),
-    "ms": _sb(448, F32), "xx": _sb(96, F32), "cw1": _sb(96, F32), "xy": _sb(64, F32),
-    "nl": _sb(64, U16), "nl1": _sb(64, U16), "nf": _sb(64, F32), "pw": _sb(32, U16),
-    "t28": _sb(28, F32), "ff": _sb(112, F32), "pr": _sb(112, F32), "p3": _sb(28, F32), "uu": _sb(56, F32),
-    "dl0": _sb(112, F32), "dl1": _sb(112, F32), "d30": _sb(28, F32), "d31": _sb(28, F32),
+    "lti": _sb(28, I32), "rti": _sb(28, I32), "pi": _sb(1, I32), "ci": _sb(28, I32), "ui": _sb(8, I32), "ki": _sb(4, I32),
+    "kf": _sb(4, F32), "kt": _sb(8, F32), "k1": _sb(4, F32), "k2": _sb(4, F32), "cl": _sb(4, U16), "cla": _sb(8, U16), "clb": _sb(8, U16),
+    "ka": _sb(64, F32), "kao": _sb(64, F32), "kb": _sb(128, F32), "kbo": _sb(128, F32),
+    "nf": _sb(56, F32), "n1": _sb(56, F32), "n2": _sb(56, F32), "n3": _sb(56, F32),
+    "sg": _sb(WIN, BF), "th": _sb(480, BF), "g1": _sb(WIN, BF), "wq": _sb(WIN, BF), "h1": _sb(WIN, BF), "ls": _sb(WIN, BF),
+    "a1": _sb(WIN, BF), "p0": _sb(WIN, BF), "p1": _sb(WIN, BF), "nm": _sb(WIN, F32),
+    "g2": _sb(448, BF), "g3": _sb(448, BF), "h2": _sb(448, BF), "ms": _sb(448, BF), "gl": _sb(896, F32),
+    "t0": _sb(TW, BF), "t1": _sb(TW, BF), "tp": _sb(TW, BF), "tm": _sb(TW, BF), "tg": _sb(1344, BF), "tf": _sb(1360, BF), "ta": _sb(448, BF),
+    "xx": _sb(96, BF), "da": _sb(168, F32), "db": _sb(168, F32), "ob": _sb(168, F32),
+    "nl": _sb(28, U16), "nl1": _sb(32, U16), "pw": _sb(32, U16),
     "ps": ("psum", [128, 4096], F32),
 }
 for _k in range(3):
@@ -91,6 +99,9 @@ def rank_program(g, core, T, topo):
     def V(name, a, b, s=1):
         return (T[name][:, a:b] if s == 1 else T[name][:, a:b:s], [(name, range(a, b, s))])
 
+    def N(name, a, n, s):
+        return V(name, a, a + (n - 1) * s + 1, s)
+
     def I(name, a, b, off, c, d):
         return (T[name][:, a:b].indirect(T[off][:, c:d]), [(name, range(a, b)), (off, range(c, d))])
 
@@ -143,11 +154,25 @@ def rank_program(g, core, T, topo):
     def fill(out, c):
         do("v", lambda e: e.memset(out[0], c), out)
 
-    def act(out, a, func=COPY, scale=1.0):
-        if isinstance(scale, tuple):
-            do("s", lambda e: e.activation(out[0], a[0], func, scale=scale[0]), out, a, scale)
+    def scan(out, d0, d1):
+        do("v", lambda e: e.tensor_tensor_scan(out[0], d0[0], d1[0], 0.0, MUL, ADD), out, d0, d1)
+
+    def act(out, a, func=COPY, scale=1.0, bias=None):
+        col = [x for x in (scale, bias) if isinstance(x, tuple)]
+        sc = scale[0] if isinstance(scale, tuple) else scale
+        if bias is None:
+            do("s", lambda e: e.activation(out[0], a[0], func, scale=sc), out, a, *col)
         else:
-            do("s", lambda e: e.activation(out[0], a[0], func, scale=scale), out, a)
+            do("s", lambda e: e.activation(out[0], a[0], func, bias=bias[0], scale=sc), out, a, *col)
+
+    def sfill(out, c):
+        act(out, V("one", 0, len(out[1][0][1])), COPY, c)
+
+    def iota(out, pattern, base, cm=0):
+        do("p", lambda e: e.iota(out[0], pattern, base, cm, allow_small_or_imprecise_dtypes=True), out)
+
+    def gcopy(out, a):
+        do("p", lambda e: e.affine_select(out[0], a[0], [[0, len(out[1][0][1])]], GE, 0.0, 0, 0), out, a)
 
     def quant(q, s, a, b, tile, ta, tb):
         do("v", lambda e: e.quantize_mx(T[q][:, a:b], T[s][:, a:b], T[tile][:, ta:tb]), [V(q, a, b), V(s, a, b)], V(tile, ta, tb))
@@ -160,53 +185,50 @@ def rank_program(g, core, T, topo):
     def PS(bank, n):
         return V("ps", 512 * bank, 512 * bank + n)
 
-    def conv2(buf, o, out):
-        tr(V("xx", 16, 80), V(buf, o + 5, o + 510, 8))
-        tr(V(buf, o + 896, o + 992), V("xx", 0, 96))
-        cp(out, I(buf, o, o + 992, "cl2", 0, 4))
+    def node(name, a=0, b=448, o=0):
+        return V(name, o + NODE + a, o + NODE + b)
 
-    def conv1(out):
-        tr(V("xy", 16, 48), V("cw1", 0, 32))
-        tr(V("cw1", 32, 96), V("xy", 0, 64))
-        cp(out, I("cw1", 0, 96, "cl1", 0, 2))
+    def leaf(name, half, o=0):
+        return N(name, o + (0 if half else WIN - 8 * 224), 224, 8)
 
-    def rewrite(plus, minus, acting, turns, base, nxt, dl, d3):
-        tt(V("ff", 1, 112, 2), plus, minus, acting)
-        for o, i, a in turns:
-            tt(o, i, a, MUL)
-        tt(V("pr", 0, 112), V("ff", 0, 112), V(dl, 0, 112), MUL)
-        tt(V("p3", 0, 28), V("ff", 0, 56, 2), V(d3, 0, 28), MUL)
-        tt(V("uu", 0, 56), V("pr", 0, 56), V("pr", 56, 112), ADD)
-        tt(V("uu", 1, 56, 2), V("uu", 1, 56, 2), V("p3", 0, 28), ADD)
-        tt(nxt, base, V("uu", 0, 56), ADD)
+    def W(name, off, c=0, d=28, o=0):
+        return I(name, o, o + WIN, off, c, d)
 
-    L0, R0, LR0 = V("tb0", 5, 448, 16), V("tb0", 13, 448, 16), V("tb0", 5, 448, 8)
-    L1, R1, LR1 = V("tt", 901, 1344, 16), V("tt", 909, 1344, 16), V("tt", 901, 1344, 8)
+    def L(t):
+        return N(t, 16, 28, 48)
 
-    def ahead_lists():
-        tr(V("tp", 0, 448), V("p0", 0, 448))
-        ts(V("cw1", 0, 28), V("tp", 4, 448, 16), 896.0, None, ADD)
-        conv1(V("pw", 0, 32))
-        tt(V("dl0", 56, 112, 2), R0, L0, SUB)
-        tt(V("dl0", 57, 112, 2), V("tp", 13, 448, 16), R0, SUB)
+    def R(t):
+        return N(t, 40, 28, 48)
 
-    def ahead_children():
-        tr(V("ta", 0, 448), V("a1", 0, 448))
-        tt(V("dl0", 0, 56), V("ta", 5, 448, 8), LR0, SUB)
-        tt(V("d30", 0, 28), L0, V("ta", 13, 448, 16), SUB)
+    def swap1(t):
+        tr(V("xx", 16, 80), N(t, 16, 64, 24))
+
+    def swap2(t):
+        tr(V(t, SW, TW), V("xx", 0, 96))
+
+    def pick(out, t, n, add):
+        ts(V(out, 0, 16 * n), I(t, 0, TW, "cl", 0, n), float(add), None, ADD)
+
+    def D(name, i):
+        return N(name, i, 28, 6)
 
     def scores(half):
         a = 224 * half
-        mm(4 + half, 224, "qk", "sk", 0, "qx", "sx", a, a + 224)
+        mm(4 + half, 224, "qa", "sa", 0, "qx", "sx", a, a + 224)
+        mm(6 + half, 224, "qb", "sb", 0, "qx", "sx", a, a + 224)
+
+    SA, SL, BA, ST, BT = V("kbo", 0, 1), V("kao", 0, 1), V("kbo", 32, 33), V("kbo", 64, 65), V("kbo", 96, 97)
 
     def signs(half):
         a = 224 * half
-        act(V("sg", a, a + 224), PS(4 + half, 224), SIGN)
-        act(V("sg", 448 + a, 672 + a), PS(4 + half, 224), SIGN, V("kf", 5, 6))
+        act(node("sg", a, a + 224), PS(4 + half, 224), SIGN, SA, BA)
+        act(leaf("sg", half), PS(4 + half, 224), SIGN, SL, BA)
+        act(V("th", a, a + 224), PS(6 + half, 224), SIGN, ST, BT)
 
-    def local_signs(half):
-        a = 224 * half
-        tr(V("tg", 896 + a, 1120 + a), V("sg", a, a + 224))
+    def child_steps(t, a, b):
+        tt(D("da", 0), a, L(t), SUB)
+        tt(D("da", 3), L(t), b, SUB)
+        tt(D("da", 4), b, R(t), SUB)
 
     dma("y", T.lti[:, 0:28], T.lt[:, :], writes=[("lti", range(28))])
     dma("s", T.rti[:, 0:28], T.rt[:, :], writes=[("rti", range(28))])
@@ -224,144 +246,174 @@ def rank_program(g, core, T, topo):
         lands("ql%d" % k, 224, "aC%d" % k, p)
         lands("sl%d" % k, 224, "aS%d" % k, p)
     do("p", lambda e: e.iota(T.pi[:, 0:1], [[0, 1]], 0, 1), V("pi", 0, 1))
-    do("p", lambda e: e.iota(T.ci[:, 0:28], [[32, 14], [0, 2]], -896, 0), V("ci", 0, 28))
+    iota(V("k1", 0, 4), [[-23, 2], [-23 * 32, 2]], SW - 16)
+    iota(V("k2", 0, 4), [[24, 2], [24 * 32, 2]], 16)
+    do("p", lambda e: e.iota(T.ci[:, 0:28], [[32, 14], [0, 2]], -224, 0), V("ci", 0, 28))
     do("p", lambda e: e.iota(T.ui[:, 0:8], [[16, 8]], 0, 0), V("ui", 0, 8))
-    do("p", lambda e: e.iota(T.k1[:, 0:4], [[7, 2], [224, 2]], 0, 0, allow_small_or_imprecise_dtypes=True), V("k1", 0, 4))
-    do("p", lambda e: e.iota(T.k2[:, 0:4], [[8, 2], [256, 2]], 5, 0, allow_small_or_imprecise_dtypes=True), V("k2", 0, 4))
+    for h in range(2):
+        iota(leaf("ls", h), [[1, 224]], 224 * h - 224)
     fill(V("one", 0, 512), 1.0)
-    for b in range(4):
-        do("p", lambda e: e.affine_select(T.et[:, 512 * b:512 * b + 512], T.one[:, 0:512], [[-1, 512]], AluOpType.is_equal, 0.0, b, 4),
-           V("et", 512 * b, 512 * b + 512), V("one", 0, 512))
-    fill(V("tb0", 0, 448), 0.0)
-    act(V("tb0", 448, 896), V("tb0", 0, 448), COPY, 0.0)
-    for name, a, b in (("xx", 0, 96), ("cw1", 0, 32), ("xy", 0, 64), ("tt", 896, 1344), ("tt", 1344, 1792), ("sg", 896, 912),
-                       ("p0", 0, 448), ("gg1", 448, 896), ("h1", 448, 896), ("p1", 0, 448)):
-        act(V(name, a, b), V("tb0", 448, 448 + b - a), COPY, 0.0)
-    for i, (s1, s2, ops) in enumerate([(15, None, (ANDB,)), (4, 1, (SHR, ANDB)), (1, None, (ANDB,)), (31, None, (ANDB,)), (3, None, (ANDB,)), (4, None, (ANDB,))]):
+    fill(V("ka", 0, 64), 0.0)
+    fill(N("t0", 1, 512, 3), 0.0)
+    for i, (s1, s2, ops) in enumerate([(15, None, (ANDB,)), (4, 1, (SHR, ANDB)), (1, None, (ANDB,)), (31, None, (ANDB,))]):
         ts(V("ki", i, i + 1), V("pi", 0, 1), s1, s2, *ops)
-    cp(V("kf", 0, 6), V("ki", 0, 6))
+    for j, q, s, c in [(0, 3, 8, 1.0), (0, 2, 16, 1.0), (1, 0, 4, 3.0), (1, 1, 8, 2.0), (1, 7, 8, 2.0)]:
+        fill(V("ka", 32 * j + q, 32 * j + 32, s), c)
+    cp(V("kf", 0, 4), V("ki", 0, 4))
+    tr(V("kao", 0, 64), V("ka", 0, 64))
+    sfill(V("xx", 0, 96), 0.0)
+    sfill(N("t1", 1, 512, 3), 0.0)
+    for j, c in enumerate([0.0, -EPS, 0.0, EPS]):
+        sfill(V("kb", 32 * j, 32 * j + 32), c)
+    for j, q, s, c in [(0, 5, 8, -1.0), (1, 0, 4, EPS), (2, 0, 8, -1.0), (3, 3, 8, -EPS), (0, 3, 8, 1.0), (1, 1, 8, EPS), (2, 4, 16, -1.0), (3, 6, 8, -EPS),
+                       (0, 2, 16, 1.0), (1, 7, 8, EPS), (2, 5, 8, -1.0), (3, 12, 16, -EPS), (1, 10, 16, EPS), (2, 7, 8, -1.0), (2, 2, 8, 1.0), (2, 1, 8, 1.0)]:
+        sfill(V("kb", 32 * j + q, 32 * j + 32, s), c)
 
     def K(i):
         return V("kt", i, i + 1)
     X_, H_, B_ = V("kf", 0, 1), V("kf", 1, 2), V("kf", 2, 3)
     tt(K(0), B_, H_, SUB)
-    ts(K(2), H_, -32.0, 925.0, MUL, ADD)
-    ts(K(4), B_, 2.0, -860.0, MUL, ADD)
+    ts(K(2), H_, -28.0, 30.0, MUL, ADD)
+    ts(K(3), X_, 48.0, None, MUL)
     tt(K(1), K(0), K(0), MUL)
-    ts(K(3), B_, -4.0, K(2), MUL, ADD)
-    ts(K(5), K(1), -1.0, None, MUL)
-    tt(K(4), K(4), K(3), ADD)
-    ts(K(3), X_, -14.0, K(3), MUL, ADD)
-    tt(K(4), K(4), K(1), MUL)
-    tt(K(3), K(3), K(1), MUL)
-    tt(K(4), K(4), X_, ADD)
-    ts(K(3), X_, 16.0, K(3), MUL, ADD)
-    ts(V("k1", 0, 4), V("k1", 0, 4), K(5), K(3), MUL, ADD)
+    ts(K(2), X_, -46.0, K(2), MUL, ADD)
+    ts(V("k2", 0, 4), V("k2", 0, 4), K(3), None, ADD)
+    ts(V("cla", 0, 8), V("ui", 0, 8), SL, None, ADD)
+    ts(V("k1", 0, 4), V("k1", 0, 4), K(2), K(1), ADD, MUL)
+    ts(V("clb", 0, 8), V("ui", 0, 8), V("kao", 32, 33), None, ADD)
     tt(V("k1", 0, 4), V("k1", 0, 4), V("k2", 0, 4), ADD)
-    cp(V("cl2", 0, 4), V("k1", 0, 4))
-    ts(V("clu", 0, 8), V("ui", 0, 8), V("kf", 4, 5), None, ADD)
-    for k in range(2):
-        ts(V("cl1", k, k + 1), K(4), 16.0 * k, None, ADD)
-    ts(V("kf", 6, 7), V("kf", 5, 6), 0.25, None, MUL)
-    ts(V("kf", 5, 6), V("kf", 5, 6), -0.25, 1.0, MUL, ADD)
-    ts(V("tb0", 4, 448, 16), V("ci", 0, 28), V("kf", 3, 4), None, ADD)
-    cp(L1, V("lti", 0, 28))
-    cp(R1, V("rti", 0, 28))
-    cp(V("nl", 0, 28), V("lti", 0, 28))
-    conv2("tt", 896, V("nf", 0, 64))
-    cp(L0, V("nf", 0, 28))
-    cp(R0, V("nf", 32, 60))
-    tr(V("ls", 0, 448), V("tb0", 0, 448))
-    act(V("ls", 448, 896), V("ls", 0, 448))
-    act(V("a1", 0, 448), I("ls", 0, 896, "nl", 0, 28))
+    ts(N("t0", 7, 28, 48), V("ci", 0, 28), V("kf", 3, 4), None, ADD)
+    cp(V("cl", 0, 4), V("k1", 0, 4))
+    fill(node("p0"), float(NONE))
+    ts(V("nf", 0, 56, 2), V("lti", 0, 28), -224.0, None, ADD)
+    ts(V("nf", 1, 56, 2), V("rti", 0, 28), -224.0, None, ADD)
+    ts(V("n1", 0, 56), V("nf", 0, 56), 7.0, -1536.0, MUL, ADD)
+    ts(V("n2", 0, 56), V("nf", 0, 56), 224.0, None, GE)
+    ts(V("n3", 0, 56), V("nf", 0, 56), 448.0, -4096.0, GE, MUL)
+    tt(V("n1", 0, 56), V("n1", 0, 56), V("n2", 0, 56), MUL)
+    tt(V("n3", 0, 56), V("n3", 0, 56), V("nf", 0, 56), ADD)
+    tt(N("t1", 16, 56, 24), V("n1", 0, 56), V("n3", 0, 56), ADD)
+    swap1("t1")
+    ts(V("nl", 0, 28), L("t1"), float(MID), None, ADD)
+    swap2("t1")
     quant("qu", "su", 0, 128, "ut", 0, 512)
-    do("v", lambda e: e.tensor_copy(T.qk[:, 0:128].bitcast(dt.uint32), T.qu[:, 0:128].bitcast(dt.uint32).indirect(T.clu[:, 0:8])),
-       V("qk", 0, 128), V("qu", 0, 128), V("clu", 0, 8))
-    do("s", lambda e: e.activation(T.sk[:, 0:128], T.su[:, 0:128].indirect(T.clu[:, 0:8]), COPY), V("sk", 0, 128), V("su", 0, 128), V("clu", 0, 8))
-    cp(I("p0", 0, 896, "nl", 0, 28), V("ls", 0, 448))
+    for e_ in range(2):
+        cp(N("t0", 16 + 24 * e_, 32, 48), I("t1", 0, TW, "cl", 2 * e_, 2 * e_ + 2))
+    tr(V("kbo", 0, 128), V("kb", 0, 128))
+    tr(node("ls"), N("t0", 1, 448, 3))
+    for name, a, n, s in (("da", 0, 168, 1), ("db", 0, 168, 1), ("tp", 1360, 8, 24), ("tm", 1360, 8, 24), ("tg", 0, 56, 24), ("tf", 5, 56, 24)):
+        sfill(N(name, a, n, s), 0.0)
+    sfill(V("th", 448, 480), 1.0)
+    act(node("a1"), W("ls", "nl"))
+    for q, s, c in (("qa", "sa", "cla"), ("qb", "sb", "clb")):
+        do("v", lambda e: e.tensor_copy(T[q][:, 0:128].bitcast(dt.uint32), T.qu[:, 0:128].bitcast(dt.uint32).indirect(T[c][:, 0:8])),
+           V(q, 0, 128), V("qu", 0, 128), V(c, 0, 8))
+        do("s", lambda e: e.activation(T[s][:, 0:128], T.su[:, 0:128].indirect(T[c][:, 0:8]), COPY), V(s, 0, 128), V("su", 0, 128), V(c, 0, 8))
+    for name in ("g1", "h1"):
+        for h in range(2):
+            iota(leaf(name, h), [[0, 224]], 0)
+    iota(node("p1"), [[0, 448]], 0)
+    cp(W("p0", "nl"), node("ls"))
     for h in range(2):
         quant("qx", "sx", 224 * h, 224 * h + 224, "xa", 896 * h, 896 * h + 896)
         scores(h)
-        if h == 0:
-            quant("qe", "se", 0, 512, "et", 0, 2048)
     for h in range(2):
         signs(h)
-    ahead_lists()
+
+    def ahead_parents():
+        tr(N("tp", 10, 448, 3), node("p0"))
+        tt(D("db", 0), R("t0"), L("t0"), SUB)
+        swap1("tp")
+        tt(D("db", 3), N("tp", 49, 28, 48), R("t0"), SUB)
+        swap2("tp")
+
+    def ahead_children():
+        tr(V("ta", 0, 448), node("a1"))
+        pick("pw", "tp", 2, 224)
+        child_steps("t0", V("ta", 5, 448, 16), V("ta", 13, 448, 16))
+
+    ahead_parents()
     ahead_children()
-    for h in range(2):
-        local_signs(h)
 
     xs, nl = ["xa", "xb"], "nl"
     for k in range(3):
         last = k == 2
         p = T.cores[rank ^ ROUNDS[k]]
         old, new = xs[k % 2], xs[(k + 1) % 2]
-        w = I("sg", 0, 896, nl, 0, 28)
-        do("s", lambda e: e.activation(T.gg1[:, 0:448], w[0], RELU, bias=T.kf[:, 6:7]), V("gg1", 0, 448), w, V("kf", 6, 7))
-        ts(V("gg3", 0, 448), I("sg", 0, 912, "pw", 0, 28), 0.75, -1.25, MUL, ADD)
-        act(V("gg2", 0, 448), I("gg1", 0, 896, nl, 0, 28))
-        tr(V("tg", 448, 896), V("gg1", 0, 448))
-        tr(V("tg", 1344, 1792), V("gg3", 0, 448))
-        tr(V("tg", 0, 448), V("gg2", 0, 448))
-        act(V("tt", 896, 1344), V("tg", 896, 1344), RELU)
-        act(V("tt", 902, 1344, 16), V("tg", 898, 1344, 16), RELU, -1.0)
+        act(V("g3", 0, 448), I("th", 0, 480, "pw", 0, 28), RELU, SA)
+        tt(node("g1"), W("sg", nl), V("th", 0, 448), GT)
+        act(V("g2", 0, 448), W("g1", nl), COPY, SA)
+        for h in range(2):
+            gcopy(leaf("wq", h), node("g1", 224 * h, 224 * h + 224))
         if k == 0:
             for b in range(4):
-                act(V("win", 896 * b, 896 * b + 448), V("xa", b, 1792, 4), COPY, 0.5)
-        else:
-            for b in range(4):
-                act(V("win", 896 * b, 896 * b + 224), V(old, b, 896, 4), COPY, 0.5)
-        rewrite(V("tg", 896, 1792, 16), V("tg", 452, 1344, 16), GT, [(V("ff", 0, 112, 2), V("ff", 1, 112, 2), V("tg", 1, 896, 16))],
-                LR0, LR1, "dl0", "d30")
-        tr(V("wq", 0, 448), V("tt", 896, 1344))
-        act(V("wq", 448, 896), V("wq", 0, 448), COPY, V("kf", 5, 6))
-        conv2("tt", 896, V("nl1", 0, 64))
-        act(V("h1", 0, 448), I("wq", 0, 896, "nl1", 0, 28))
-        act(V("h2", 0, 448), I("h1", 0, 896, "nl1", 0, 28))
-        cp(I("p1", 0, 896, "nl1", 0, 28), V("wq", 0, 448))
-        if k == 0:
-            for b in range(4):
-                act(V("win", 896 * b + 448, 896 * b + 896), V("lvt", b, 1792, 4), COPY, 0.5)
-        else:
-            for b in range(4):
-                act(V("win", 896 * b + 448, 896 * b + 672), PS(b, 224), COPY, 0.5)
+                do("p", lambda e: e.affine_select(T.et[:, 512 * b:512 * b + 512], T.one[:, 0:512], [[-1, 512]], AluOpType.is_equal, 0.0, b, 4),
+                   V("et", 512 * b, 512 * b + 512), V("one", 0, 512))
+        if k == 1:
+            iota(node("nm"), [[1, 448]], 0)
+            for h in range(2):
+                iota(leaf("nm", h), [[1, 224]], 448 + 224 * h)
+        tr(N("tg", 1, 448, 3), V("g3", 0, 448))
+        tr(N("tg", 2, 448, 3), node("g1"))
+        scan(V("ob", 0, 168), N("tg", 0, 168, 8), V("db", 0, 168))
+        for o, i, s in ((1, 2, 12), (19, 5, 24), (22, 23, 24)):
+            act(V("t1", o, 1344, s), V("tg", i, 1344, s))
+        tt(V("da", 2, 168, 3), V("ob", 2, 168, 3), N("t0", 16, 56, 24), ADD)
+        tr(N("tg", 0, 448, 3), V("g2", 0, 448))
+        scan(N("t1", 0, 168, 8), N("tg", 1, 168, 8), V("da", 0, 168))
+        for b in range(4):
+            act(node("win", 0, 448 if k == 0 else 224, WIN * b), V(old, b, 1792 if k == 0 else 896, 4), COPY, 0.5)
+        swap1("t1")
+        tr(node("wq"), N("t1", 1, 448, 3))
+        swap2("t1")
+        tt(D("db", 0), R("t1"), L("t1"), SUB)
+        pick("nl1", "t1", 2, MID)
+        act(node("h1"), W("wq", "nl1"))
+        act(V("h2", 0, 448), W("h1", "nl1"), ActivationFunctionType.Abs, ST)
+        cp(W("p1", "nl1"), node("wq"))
+        for b in range(4):
+            if k == 0:
+                for h in range(2):
+                    act(leaf("win", h, WIN * b), V("lvt", 896 * h + b, 896 * h + 896, 4), COPY, 0.5)
+            else:
+                act(leaf("win", 0, WIN * b), PS(b, 224), COPY, 0.5)
         if not last:
-            act(V("p0", 0, 448), V("wq", 0, 448), COPY, 0.0)
-        tt(V("dl1", 56, 112, 2), R1, L1, SUB)
-        tr(V("tt", 448, 896), V("h1", 0, 448))
-        tt(V("dl1", 0, 56), V("tt", 453, 896, 8), LR1, SUB)
-        tt(V("d31", 0, 28), L1, V("tt", 461, 896, 16), SUB)
-        tr(V("tg2", 0, 448), V("h2", 0, 448))
-        tr(V("tt", 1344, 1792), V("p1", 0, 448))
-        tt(V("dl1", 57, 112, 2), V("tt", 1357, 1792, 16), R1, SUB)
-        rewrite(V("tt", 898, 1792, 16), V("tt", 454, 1344, 16), MUL,
-                [(V("ff", 0, 56, 2), V("ff", 1, 56, 2), V("tg2", 3, 448, 16)), (V("ff", 56, 112, 2), V("ff", 57, 112, 2), V("tt", 451, 896, 16))],
-                LR1, LR0, "dl1", "d31")
+            iota(node("p0"), [[0, 448]], NONE)
+        tr(N("tf", 1, 448, 3), node("h1"))
+        tr(N("tf", 0, 448, 3), node("p1"))
+        tt(N("tf", 19, 56, 24), N("tf", 19, 56, 24), N("tg", 23, 56, 24), MUL)
+        tt(N("tf", 21, 56, 24), N("tf", 21, 56, 24), N("tg", 5, 56, 24), MUL)
+        tt(D("db", 3), N("tf", 39, 28, 48), R("t1"), SUB)
+        tr(N("tf", 11, 448, 3), V("h2", 0, 448))
+        scan(V("ob", 0, 168), N("tf", 5, 168, 8), V("db", 0, 168))
+        child_steps("t1", L("tf"), R("tf"))
+        tt(V("da", 2, 168, 3), V("ob", 2, 168, 3), N("t1", 16, 56, 24), ADD)
+        scan(N("t0", 0, 168, 8), N("tf", 3, 168, 8), V("da", 0, 168))
         nl = "rc%d" % k
-        conv2("tb0", 0, V(nl, 0, 64))
+        swap1("t0")
+        tr(node("ls"), N("t0", 1, 448, 3))
+        swap2("t0")
+        pick(nl, "t0", 4, MID)
         send(p, T["lr%d" % k][:, 0:28], T[nl][:, 32:60], "aR%d" % k, V(nl, 32, 60))
-        tr(V("ls", 0, 448), V("tb0", 0, 448))
         for h, (c0, c1) in enumerate(PARTS):
             for b in range(4):
-                act(V("zr", 448 * b + c0, 448 * b + c1), I("win", 896 * b, 896 * b + 896, nl, 32 + c0 // 16, 32 + c1 // 16))
+                act(V("zr", 448 * b + c0, 448 * b + c1), W("win", nl, 32 + c0 // 16, 32 + c1 // 16, WIN * b))
             if h == 0:
-                act(V("ls", 448, 896), V("ls", 0, 448))
+                act(node("a1"), W("ls", nl))
+                for i in range(2):
+                    gcopy(leaf("a1", i), node("a1", 224 * i, 224 * i + 224))
         for h, (c0, c1) in enumerate(PARTS):
             for b in range(4):
-                o, w = V("zt", 4 * c0 + b, 4 * c1, 4), I("win", 896 * b, 896 * b + 896, nl, c0 // 16, c1 // 16)
-                tt(o, w, V("zr", 448 * b + c0, 448 * b + c1), ADD)
+                tt(V("zt", 4 * c0 + b, 4 * c1, 4), W("win", nl, c0 // 16, c1 // 16, WIN * b), V("zr", 448 * b + c0, 448 * b + c1), ADD)
             quant("qz", "sz", c0, c1, "zt", 4 * c0, 4 * c1)
             for b in range(4):
                 mm(4 * h + b, c1 - c0, "qw", "sw", 128 * b, "qz", "sz", c0, c1)
-        if last:
-            for i, q in enumerate((5, 13)):
-                dma("y", T.gr[:, 448 * i:448 * i + 448], T.ls[q:128:16, 0:448], reads=[("ls", range(448))])
-        act(V("ms", 0, 448), I("ls", 0, 896, "lr%d" % k, 0, 28))
-        tr(V("tm", 0, 448), V("ms", 0, 448))
-        ts(V("t28", 0, 28), V("tm", 5, 448, 16), 448.0, -448.0, GE, MUL)
-        tt(V("cw1", 0, 28), V("tm", 5, 448, 16), V("t28", 0, 28), ADD)
         mu, lm = "mu%d" % k, "lm%d" % k
-        conv1(V(mu, 0, 32))
+        act(V("ms", 0, 448), W("a1", "lr%d" % k))
+        tr(N("tm", 10, 448, 3), V("ms", 0, 448))
+        swap1("tm")
+        swap2("tm")
+        pick(mu, "tm", 2, 224)
         send(p, T[lm][:, 0:14], T[mu][:, 14:28], "aM%d" % k, V(mu, 14, 28))
         for h, (c0, c1) in enumerate(PARTS):
             for b in range(4):
@@ -381,22 +433,25 @@ def rank_program(g, core, T, topo):
         send(p, T[ql][:, 0:224].bitcast(dt.uint8), T[qs][:, 0:224].bitcast(dt.uint8), "aC%d" % k, V(qs, 0, 224))
         send(p, T[sl][:, 0:224], T[ss][:, 0:224], "aS%d" % k, V(ss, 0, 224))
         if not last:
-            cp(I("p0", 0, 896, nl, 0, 28), V("ls", 0, 448))
-            act(V("a1", 0, 448), I("ls", 0, 896, nl, 0, 28))
+            iota(node("p1"), [[0, 448]], 0)
+            cp(W("p0", nl), node("ls"))
+        if k == 0:
+            quant("qe", "se", 0, 512, "et", 0, 2048)
         for b in range(4):
             tt(V(new, 896 + b, 1792, 4), I("hw", 448 * b, 448 * b + 448, lm, 0, 14), V(old, 896 + b, 1792, 4), ADD)
         quant("qx", "sx", 224, 448, new, 896, 1792)
         if not last:
             scores(1)
-            ahead_lists()
+            ahead_parents()
             for b in range(4):
-                act(V("win", 896 * b + 672, 896 * b + 896), I("hw", 448 * b, 448 * b + 448, lm, 0, 14), COPY, 0.5)
-            for b in range(4):
-                act(V("win", 896 * b + 224, 896 * b + 448), V(new, 896 + b, 1792, 4), COPY, 0.5)
+                act(leaf("win", 1, WIN * b), I("hw", 448 * b, 448 * b + 448, lm, 0, 14), COPY, 0.5)
             signs(1)
-            local_signs(1)
-            act(V("p1", 0, 448), V("ls", 0, 448), COPY, 0.0)
+            for b in range(4):
+                act(node("win", 224, 448, WIN * b), V(new, 896 + b, 1792, 4), COPY, 0.5)
         else:
+            for i in range(2):
+                act(V("gl", 448 * i, 448 * i + 448), W("nm", nl, 32 * i, 32 * i + 28))
+            dma("y", T.gr[:, :], T.gl[0:128:16, 0:896], reads=[("gl", range(896))])
             quant("qv", "sv", 0, 128, "vt", 0, 512)
             finish(mm, act, dma, V, PS, T, 1)
         for b in range(4):
@@ -408,7 +463,6 @@ def rank_program(g, core, T, topo):
             scores(0)
             signs(0)
             ahead_children()
-            local_signs(0)
         else:
             finish(mm, act, dma, V, PS, T, 0)
     for q in "vstp":

@@ -1,7 +1,7 @@
 from concourse.mybir import dt, AluOpType, ActivationFunctionType
 
 ROUNDS = [1, 2, 3]
-PARTS = [(0, 256), (256, 448)]
+PARTS = [(0, 320), (320, 448)]
 ADD, SUB, MUL = AluOpType.add, AluOpType.subtract, AluOpType.mult
 GE, GT, MAX = AluOpType.is_ge, AluOpType.is_gt, AluOpType.max
 ANDB, SHR = AluOpType.bitwise_and, AluOpType.arith_shift_right
@@ -29,7 +29,7 @@ SCRATCH = {
     "qz": _sb(448, MXC), "sz": _sb(448, U8),
     "lti": _sb(28, I32), "rti": _sb(28, I32), "pi": _sb(1, I32), "ci": _sb(28, I32), "ui": _sb(8, I32), "ki": _sb(4, I32),
     "kf": _sb(4, F32), "kt": _sb(8, F32), "k1": _sb(4, F32), "k2": _sb(4, F32), "cl": _sb(4, U16), "cla": _sb(8, U16), "clb": _sb(8, U16),
-    "ka": _sb(64, F32), "kao": _sb(64, F32), "kb": _sb(128, F32), "kbo": _sb(128, F32),
+    "kb": _sb(160, F32), "kbo": _sb(160, F32),
     "nf": _sb(56, F32), "n1": _sb(56, F32), "n2": _sb(56, F32), "n3": _sb(56, F32),
     "sg": _sb(WIN, BF), "th": _sb(480, BF), "g1": _sb(WIN, BF), "wq": _sb(WIN, BF), "h1": _sb(WIN, BF), "ls": _sb(WIN, BF),
     "a1": _sb(WIN, BF), "p0": _sb(WIN, BF), "p1": _sb(WIN, BF), "nm": _sb(WIN, F32),
@@ -72,8 +72,6 @@ def rank_program(g, core, T, topo):
                     if rsrc == src or not (cols & rcols):
                         continue
                 elif not (wr or rwr) or not (cols & rcols):
-                    continue
-                elif rsrc == src and not rwr:
                     continue
                 w[sem] = max(w.get(sem, 0), val)
         for sem in sorted(w):
@@ -217,13 +215,17 @@ def rank_program(g, core, T, topo):
         mm(4 + half, 224, "qa", "sa", 0, "qx", "sx", a, a + 224)
         mm(6 + half, 224, "qb", "sb", 0, "qx", "sx", a, a + 224)
 
-    SA, SL, BA, ST, BT = V("kbo", 0, 1), V("kao", 0, 1), V("kbo", 32, 33), V("kbo", 64, 65), V("kbo", 96, 97)
+    SA, BA, ST, BT, KB = [V("kbo", 32 * j, 32 * j + 1) for j in range(5)]
+    SL, B3 = V("kt", 4, 5), V("kt", 5, 6)
 
     def signs(half):
         a = 224 * half
         act(node("sg", a, a + 224), PS(4 + half, 224), SIGN, SA, BA)
         act(leaf("sg", half), PS(4 + half, 224), SIGN, SL, BA)
-        act(V("th", a, a + 224), PS(6 + half, 224), SIGN, ST, BT)
+
+    def own_tests(half):
+        a = 224 * half
+        ts(V("th", a, a + 224), PS(6 + half, 224), ST, BT, MUL, GE)
 
     def child_steps(t, a, b):
         tt(D("da", 0), a, L(t), SUB)
@@ -232,10 +234,11 @@ def rank_program(g, core, T, topo):
 
     dma("y", T.lti[:, 0:28], T.lt[:, :], writes=[("lti", range(28))])
     dma("s", T.rti[:, 0:28], T.rt[:, :], writes=[("rti", range(28))])
-    dma("s", T.ut[:, :], T.u[:, :], writes=[("ut", range(512))])
+    dma("y", T.ut[:, :], T.u[:, :], writes=[("ut", range(512))])
     for h in range(2):
-        dma("y", T.xa[:, 896 * h:896 * h + 896], T.x[:, 896 * h:896 * h + 896], writes=[("xa", range(896 * h, 896 * h + 896))])
-    dma("s", T.lvt[:, :], T.lv[:, :], writes=[("lvt", range(1792))])
+        dma("sy"[h], T.xa[:, 896 * h:896 * h + 896], T.x[:, 896 * h:896 * h + 896], writes=[("xa", range(896 * h, 896 * h + 896))])
+    need("y", "dma", acc(V("xa", 0, 1792)), [])
+    dma("y", T.lvt[:, :], T.lv[:, :], writes=[("lvt", range(1792))])
     dma("y", T.qw[:, 0:512].bitcast(dt.uint8), T.wc[:, :], writes=[("qw", range(512))])
     dma("y", T.sw[:, 0:512], T.ws[:, :], writes=[("sw", range(512))])
     dma("y", T.vt[:, :], T.v[:, :], writes=[("vt", range(512))])
@@ -253,21 +256,18 @@ def rank_program(g, core, T, topo):
     for h in range(2):
         iota(leaf("ls", h), [[1, 224]], 224 * h - 224)
     fill(V("one", 0, 512), 1.0)
-    fill(V("ka", 0, 64), 0.0)
-    fill(N("t0", 1, 512, 3), 0.0)
+    fill(V("kb", 0, 160), 0.0)
     for i, (s1, s2, ops) in enumerate([(15, None, (ANDB,)), (4, 1, (SHR, ANDB)), (1, None, (ANDB,)), (31, None, (ANDB,))]):
         ts(V("ki", i, i + 1), V("pi", 0, 1), s1, s2, *ops)
-    for j, q, s, c in [(0, 3, 8, 1.0), (0, 2, 16, 1.0), (1, 0, 4, 3.0), (1, 1, 8, 2.0), (1, 7, 8, 2.0)]:
-        fill(V("ka", 32 * j + q, 32 * j + 32, s), c)
+    fill(V("xx", 0, 96), 0.0)
     cp(V("kf", 0, 4), V("ki", 0, 4))
-    tr(V("kao", 0, 64), V("ka", 0, 64))
-    sfill(V("xx", 0, 96), 0.0)
-    sfill(N("t1", 1, 512, 3), 0.0)
-    for j, c in enumerate([0.0, -EPS, 0.0, EPS]):
-        sfill(V("kb", 32 * j, 32 * j + 32), c)
-    for j, q, s, c in [(0, 5, 8, -1.0), (1, 0, 4, EPS), (2, 0, 8, -1.0), (3, 3, 8, -EPS), (0, 3, 8, 1.0), (1, 1, 8, EPS), (2, 4, 16, -1.0), (3, 6, 8, -EPS),
-                       (0, 2, 16, 1.0), (1, 7, 8, EPS), (2, 5, 8, -1.0), (3, 12, 16, -EPS), (1, 10, 16, EPS), (2, 7, 8, -1.0), (2, 2, 8, 1.0), (2, 1, 8, 1.0)]:
+    fill(node("p0"), float(NONE))
+    for j, q, s, c in [(1, 0, 1, -EPS), (0, 5, 8, -1.0), (0, 3, 8, 1.0), (0, 2, 16, 1.0), (4, 0, 4, 3.0), (4, 1, 8, 2.0), (4, 7, 8, 2.0),
+                       (1, 0, 4, EPS), (1, 1, 8, EPS), (1, 7, 8, EPS), (1, 10, 16, EPS), (3, 3, 8, 1.0), (3, 6, 8, 1.0), (3, 12, 16, 1.0),
+                       (2, 0, 8, -1.0), (2, 4, 16, -1.0), (2, 5, 8, -1.0), (2, 7, 8, -1.0), (2, 2, 8, 1.0), (2, 1, 8, 1.0)]:
         sfill(V("kb", 32 * j + q, 32 * j + 32, s), c)
+    sfill(N("t1", 1, 512, 3), 0.0)
+    sfill(N("t0", 1, 512, 3), 0.0)
 
     def K(i):
         return V("kt", i, i + 1)
@@ -278,70 +278,70 @@ def rank_program(g, core, T, topo):
     tt(K(1), K(0), K(0), MUL)
     ts(K(2), X_, -46.0, K(2), MUL, ADD)
     ts(V("k2", 0, 4), V("k2", 0, 4), K(3), None, ADD)
-    ts(V("cla", 0, 8), V("ui", 0, 8), SL, None, ADD)
     ts(V("k1", 0, 4), V("k1", 0, 4), K(2), K(1), ADD, MUL)
-    ts(V("clb", 0, 8), V("ui", 0, 8), V("kao", 32, 33), None, ADD)
-    tt(V("k1", 0, 4), V("k1", 0, 4), V("k2", 0, 4), ADD)
-    ts(N("t0", 7, 28, 48), V("ci", 0, 28), V("kf", 3, 4), None, ADD)
-    cp(V("cl", 0, 4), V("k1", 0, 4))
-    fill(node("p0"), float(NONE))
     ts(V("nf", 0, 56, 2), V("lti", 0, 28), -224.0, None, ADD)
     ts(V("nf", 1, 56, 2), V("rti", 0, 28), -224.0, None, ADD)
+    tt(V("k1", 0, 4), V("k1", 0, 4), V("k2", 0, 4), ADD)
+    tr(V("kbo", 0, 160), V("kb", 0, 160))
     ts(V("n1", 0, 56), V("nf", 0, 56), 7.0, -1536.0, MUL, ADD)
     ts(V("n2", 0, 56), V("nf", 0, 56), 224.0, None, GE)
     ts(V("n3", 0, 56), V("nf", 0, 56), 448.0, -4096.0, GE, MUL)
+    cp(V("cl", 0, 4), V("k1", 0, 4))
+    ts(SL, SA, 0.0, None, MAX)
     tt(V("n1", 0, 56), V("n1", 0, 56), V("n2", 0, 56), MUL)
     tt(V("n3", 0, 56), V("n3", 0, 56), V("nf", 0, 56), ADD)
+    ts(V("cla", 0, 8), V("ui", 0, 8), SL, None, ADD)
+    ts(V("clb", 0, 8), V("ui", 0, 8), KB, None, ADD)
+    tt(B3, SA, SA, MUL)
     tt(N("t1", 16, 56, 24), V("n1", 0, 56), V("n3", 0, 56), ADD)
     swap1("t1")
     ts(V("nl", 0, 28), L("t1"), float(MID), None, ADD)
+    ts(N("t0", 7, 28, 48), V("ci", 0, 28), V("kf", 3, 4), None, ADD)
     swap2("t1")
     quant("qu", "su", 0, 128, "ut", 0, 512)
-    for e_ in range(2):
-        cp(N("t0", 16 + 24 * e_, 32, 48), I("t1", 0, TW, "cl", 2 * e_, 2 * e_ + 2))
-    tr(V("kbo", 0, 128), V("kb", 0, 128))
-    tr(node("ls"), N("t0", 1, 448, 3))
-    for name, a, n, s in (("da", 0, 168, 1), ("db", 0, 168, 1), ("tp", 1360, 8, 24), ("tm", 1360, 8, 24), ("tg", 0, 56, 24), ("tf", 5, 56, 24)):
-        sfill(N(name, a, n, s), 0.0)
-    sfill(V("th", 448, 480), 1.0)
-    act(node("a1"), W("ls", "nl"))
-    for q, s, c in (("qa", "sa", "cla"), ("qb", "sb", "clb")):
+
+    def deciding(q, s, c):
         do("v", lambda e: e.tensor_copy(T[q][:, 0:128].bitcast(dt.uint32), T.qu[:, 0:128].bitcast(dt.uint32).indirect(T[c][:, 0:8])),
            V(q, 0, 128), V("qu", 0, 128), V(c, 0, 8))
         do("s", lambda e: e.activation(T[s][:, 0:128], T.su[:, 0:128].indirect(T[c][:, 0:8]), COPY), V(s, 0, 128), V("su", 0, 128), V(c, 0, 8))
+
+    for name, a, n, s in (("da", 0, 168, 1), ("db", 0, 168, 1), ("tp", 1360, 8, 24), ("tm", 1360, 8, 24), ("tg", 0, 56, 24), ("tf", 5, 56, 24)):
+        sfill(N(name, a, n, s), 0.0)
+    sfill(V("th", 448, 480), 1.0)
+    for e_ in range(2):
+        cp(N("t0", 16 + 24 * e_, 32, 48), I("t1", 0, TW, "cl", 2 * e_, 2 * e_ + 2))
+    deciding("qa", "sa", "cla")
+    tr(node("ls"), N("t0", 1, 448, 3))
+    deciding("qb", "sb", "clb")
+    act(node("a1"), W("ls", "nl"))
     for name in ("g1", "h1"):
         for h in range(2):
             iota(leaf(name, h), [[0, 224]], 0)
     iota(node("p1"), [[0, 448]], 0)
-    cp(W("p0", "nl"), node("ls"))
+    tt(D("db", 0), R("t0"), L("t0"), SUB)
+    cp(W("p0", "nl", 0, 14), node("ls", 0, 224))
     for h in range(2):
         quant("qx", "sx", 224 * h, 224 * h + 224, "xa", 896 * h, 896 * h + 896)
         scores(h)
-    for h in range(2):
         signs(h)
-
-    def ahead_parents():
-        tr(N("tp", 10, 448, 3), node("p0"))
-        tt(D("db", 0), R("t0"), L("t0"), SUB)
-        swap1("tp")
-        tt(D("db", 3), N("tp", 49, 28, 48), R("t0"), SUB)
-        swap2("tp")
-
-    def ahead_children():
-        tr(V("ta", 0, 448), node("a1"))
-        pick("pw", "tp", 2, 224)
-        child_steps("t0", V("ta", 5, 448, 16), V("ta", 13, 448, 16))
-
-    ahead_parents()
-    ahead_children()
+    cp(W("p0", "nl", 14, 28), node("ls", 224, 448))
+    tr(V("ta", 0, 448), node("a1"))
+    tr(N("tp", 10, 448, 3), node("p0"))
+    own_tests(0)
+    swap1("tp")
+    own_tests(1)
+    swap2("tp")
+    tt(D("db", 3), N("tp", 49, 28, 48), R("t0"), SUB)
+    pick("pw", "tp", 2, 224)
 
     xs, nl = ["xa", "xb"], "nl"
     for k in range(3):
         last = k == 2
         p = T.cores[rank ^ ROUNDS[k]]
         old, new = xs[k % 2], xs[(k + 1) % 2]
-        act(V("g3", 0, 448), I("th", 0, 480, "pw", 0, 28), RELU, SA)
+        act(V("g3", 0, 448), I("th", 0, 480, "pw", 0, 28), RELU, SA, B3)
         tt(node("g1"), W("sg", nl), V("th", 0, 448), GT)
+        child_steps("t0", V("ta", 5, 448, 16), V("ta", 13, 448, 16))
         act(V("g2", 0, 448), W("g1", nl), COPY, SA)
         for h in range(2):
             gcopy(leaf("wq", h), node("g1", 224 * h, 224 * h + 224))
@@ -382,46 +382,76 @@ def rank_program(g, core, T, topo):
         tr(N("tf", 1, 448, 3), node("h1"))
         tr(N("tf", 0, 448, 3), node("p1"))
         tt(N("tf", 19, 56, 24), N("tf", 19, 56, 24), N("tg", 23, 56, 24), MUL)
+        tt(D("da", 0), L("tf"), L("t1"), SUB)
         tt(N("tf", 21, 56, 24), N("tf", 21, 56, 24), N("tg", 5, 56, 24), MUL)
         tt(D("db", 3), N("tf", 39, 28, 48), R("t1"), SUB)
-        tr(N("tf", 11, 448, 3), V("h2", 0, 448))
+        tt(D("da", 3), L("t1"), R("tf"), SUB)
+        tt(D("da", 4), R("tf"), R("t1"), SUB)
         scan(V("ob", 0, 168), N("tf", 5, 168, 8), V("db", 0, 168))
-        child_steps("t1", L("tf"), R("tf"))
         tt(V("da", 2, 168, 3), V("ob", 2, 168, 3), N("t1", 16, 56, 24), ADD)
+        tr(N("tf", 11, 448, 3), V("h2", 0, 448))
         scan(N("t0", 0, 168, 8), N("tf", 3, 168, 8), V("da", 0, 168))
-        nl = "rc%d" % k
+        nl, mu, lm = "rc%d" % k, "mu%d" % k, "lm%d" % k
         swap1("t0")
         tr(node("ls"), N("t0", 1, 448, 3))
         swap2("t0")
+        if not last:
+            tt(D("db", 0), R("t0"), L("t0"), SUB)
         pick(nl, "t0", 4, MID)
         send(p, T["lr%d" % k][:, 0:28], T[nl][:, 32:60], "aR%d" % k, V(nl, 32, 60))
-        for h, (c0, c1) in enumerate(PARTS):
+
+        def zr(h):
+            c0, c1 = PARTS[h]
             for b in range(4):
                 act(V("zr", 448 * b + c0, 448 * b + c1), W("win", nl, 32 + c0 // 16, 32 + c1 // 16, WIN * b))
-            if h == 0:
-                act(node("a1"), W("ls", nl))
-                for i in range(2):
-                    gcopy(leaf("a1", i), node("a1", 224 * i, 224 * i + 224))
-        for h, (c0, c1) in enumerate(PARTS):
-            for b in range(4):
-                tt(V("zt", 4 * c0 + b, 4 * c1, 4), W("win", nl, c0 // 16, c1 // 16, WIN * b), V("zr", 448 * b + c0, 448 * b + c1), ADD)
+
+        def zt(h, b):
+            c0, c1 = PARTS[h]
+            tt(V("zt", 4 * c0 + b, 4 * c1, 4), W("win", nl, c0 // 16, c1 // 16, WIN * b), V("zr", 448 * b + c0, 448 * b + c1), ADD)
+
+        def layer(h):
+            c0, c1 = PARTS[h]
             quant("qz", "sz", c0, c1, "zt", 4 * c0, 4 * c1)
             for b in range(4):
                 mm(4 * h + b, c1 - c0, "qw", "sw", 128 * b, "qz", "sz", c0, c1)
-        mu, lm = "mu%d" % k, "lm%d" % k
+
+        def hw(h, b, q):
+            c0, c1 = PARTS[h]
+            o, i = V("hw", 448 * b + c0, 448 * b + c1), PS(4 * h + b, c1 - c0)
+            if q == "s":
+                act(o, i, COPY, 0.03125)
+            else:
+                ts(o, i, 0.03125, None, MUL)
+
+        zr(0)
+        cp(node("a1"), W("ls", nl))
+        for i in range(2):
+            gcopy(leaf("a1", i), node("a1", 224 * i, 224 * i + 224))
+        zr(1)
         act(V("ms", 0, 448), W("a1", "lr%d" % k))
+        for b in range(4):
+            zt(0, b)
+        zt(1, 0)
+        layer(0)
+        for b in range(1, 4):
+            zt(1, b)
+        if k == 0:
+            tr(V("ta", 0, 448), node("a1"))
+            layer(1)
+            quant("qe", "se", 0, 512, "et", 0, 2048)
         tr(N("tm", 10, 448, 3), V("ms", 0, 448))
+        if k > 0:
+            layer(1)
         swap1("tm")
+        hw(0, 0, "v")
         swap2("tm")
+        for b in range(1, 4):
+            hw(0, b, "s")
+        hw(1, 0, "v")
         pick(mu, "tm", 2, 224)
         send(p, T[lm][:, 0:14], T[mu][:, 14:28], "aM%d" % k, V(mu, 14, 28))
-        for h, (c0, c1) in enumerate(PARTS):
-            for b in range(4):
-                o, i = V("hw", 448 * b + c0, 448 * b + c1), PS(4 * h + b, c1 - c0)
-                if h == 0 or b % 2:
-                    act(o, i, COPY, 0.03125)
-                else:
-                    ts(o, i, 0.03125, None, MUL)
+        for b in range(1, 4):
+            hw(1, b, "vs"[b % 2])
         for b in range(4):
             o, w = V("sh", b, 896, 4), I("hw", 448 * b, 448 * b + 448, mu, 0, 14)
             if b % 2:
@@ -434,35 +464,46 @@ def rank_program(g, core, T, topo):
         send(p, T[sl][:, 0:224], T[ss][:, 0:224], "aS%d" % k, V(ss, 0, 224))
         if not last:
             iota(node("p1"), [[0, 448]], 0)
-            cp(W("p0", nl), node("ls"))
-        if k == 0:
-            quant("qe", "se", 0, 512, "et", 0, 2048)
+            cp(W("p0", nl, 0, 14), node("ls", 0, 224))
         for b in range(4):
             tt(V(new, 896 + b, 1792, 4), I("hw", 448 * b, 448 * b + 448, lm, 0, 14), V(old, 896 + b, 1792, 4), ADD)
+        if not last:
+            cp(W("p0", nl, 14, 18), node("ls", 224, 288))
         quant("qx", "sx", 224, 448, new, 896, 1792)
         if not last:
+            cp(W("p0", nl, 18, 28), node("ls", 288, 448))
+            for b in range(4):
+                mm(b, 224, "qe", "se", 128 * b, ql, sl, 0, 224)
             scores(1)
-            ahead_parents()
             for b in range(4):
                 act(leaf("win", 1, WIN * b), I("hw", 448 * b, 448 * b + 448, lm, 0, 14), COPY, 0.5)
-            signs(1)
             for b in range(4):
                 act(node("win", 224, 448, WIN * b), V(new, 896 + b, 1792, 4), COPY, 0.5)
+            signs(1)
         else:
             for i in range(2):
                 act(V("gl", 448 * i, 448 * i + 448), W("nm", nl, 32 * i, 32 * i + 28))
             dma("y", T.gr[:, :], T.gl[0:128:16, 0:896], reads=[("gl", range(896))])
             quant("qv", "sv", 0, 128, "vt", 0, 512)
             finish(mm, act, dma, V, PS, T, 1)
-        for b in range(4):
-            mm(b, 224, "qe", "se", 128 * b, ql, sl, 0, 224)
+            for b in range(4):
+                mm(b, 224, "qe", "se", 128 * b, ql, sl, 0, 224)
         for b in range(4):
             tt(V(new, b, 896, 4), V(old, b, 896, 4), PS(b, 224), ADD)
+        if not last:
+            tr(N("tp", 10, 448, 3), node("p0"))
         quant("qx", "sx", 0, 224, new, 0, 896)
         if not last:
             scores(0)
             signs(0)
-            ahead_children()
+            swap1("tp")
+            if k > 0:
+                tr(V("ta", 0, 448), node("a1"))
+            own_tests(1)
+            swap2("tp")
+            tt(D("db", 3), N("tp", 49, 28, 48), R("t0"), SUB)
+            pick("pw", "tp", 2, 224)
+            own_tests(0)
         else:
             finish(mm, act, dma, V, PS, T, 0)
     for q in "vstp":

@@ -2,10 +2,10 @@ from concourse.mybir import dt, AluOpType, ActivationFunctionType
 
 ROUNDS = [1, 2, 3]
 PARTS = [(0, 320), (320, 448)]
+FAR = [(0, 0, 224)] + [(b, 0, 128) for b in (1, 2, 3)] + [(b, 128, 224) for b in (1, 2, 3)]
 ADD, SUB, MUL = AluOpType.add, AluOpType.subtract, AluOpType.mult
 GE, GT, MAX = AluOpType.is_ge, AluOpType.is_gt, AluOpType.max
-ANDB, SHR = AluOpType.bitwise_and, AluOpType.arith_shift_right
-COPY, RELU, SIGN = ActivationFunctionType.Copy, ActivationFunctionType.Relu, ActivationFunctionType.Sign
+COPY, ABS, SIGN = ActivationFunctionType.Copy, ActivationFunctionType.Abs, ActivationFunctionType.Sign
 F32, BF, I32, U16, U8, MXC = "float32", "bfloat16", "int32", "uint16", "uint8", "float8_e4m3fn_x4"
 EPS = 2.0 ** -93
 WIN, MID = 4096, 2048
@@ -27,15 +27,15 @@ SCRATCH = {
     "qv": _sb(128, MXC), "sv": _sb(128, U8),
     "qe": _sb(512, MXC), "se": _sb(512, U8), "qw": _sb(512, MXC), "sw": _sb(512, U8), "qx": _sb(448, MXC), "sx": _sb(448, U8),
     "qz": _sb(448, MXC), "sz": _sb(448, U8),
-    "lti": _sb(28, I32), "rti": _sb(28, I32), "pi": _sb(1, I32), "ci": _sb(28, I32), "ui": _sb(8, I32), "ki": _sb(4, I32),
-    "kf": _sb(4, F32), "kt": _sb(8, F32), "k1": _sb(4, F32), "k2": _sb(4, F32), "cl": _sb(4, U16), "cla": _sb(8, U16), "clb": _sb(8, U16),
-    "kb": _sb(160, F32), "kbo": _sb(160, F32),
+    "li": _sb(56, I32), "ci": _sb(28, F32), "ui": _sb(8, F32),
+    "kt": _sb(4, F32), "k1": _sb(4, F32), "k2": _sb(4, F32), "cl": _sb(4, U16), "cla": _sb(8, U16), "clb": _sb(8, U16),
+    "kb": _sb(288, F32), "kbo": _sb(288, F32),
     "nf": _sb(56, F32), "n1": _sb(56, F32), "n2": _sb(56, F32), "n3": _sb(56, F32),
     "sg": _sb(WIN, BF), "th": _sb(480, BF), "g1": _sb(WIN, BF), "wq": _sb(WIN, BF), "h1": _sb(WIN, BF), "ls": _sb(WIN, BF),
     "a1": _sb(WIN, BF), "p0": _sb(WIN, BF), "p1": _sb(WIN, BF), "nm": _sb(WIN, F32),
     "g2": _sb(448, BF), "g3": _sb(448, BF), "h2": _sb(448, BF), "ms": _sb(448, BF), "gl": _sb(896, F32),
-    "t0": _sb(TW, BF), "t1": _sb(TW, BF), "tp": _sb(TW, BF), "tm": _sb(TW, BF), "tg": _sb(1344, BF), "tf": _sb(1360, BF), "ta": _sb(448, BF),
-    "xx": _sb(96, BF), "da": _sb(168, F32), "db": _sb(168, F32), "ob": _sb(168, F32),
+    "t0": _sb(TW, BF), "t1": _sb(TW, BF), "tp": _sb(TW, BF), "tm": _sb(TW, BF), "tg": _sb(1344, BF), "tf": _sb(1344, BF), "te": _sb(1360, BF), "ta": _sb(448, BF),
+    "xx": _sb(96, BF), "da": _sb(168, F32), "db": _sb(168, F32), "dc": _sb(168, F32), "dd": _sb(168, F32), "oa": _sb(168, F32), "ob": _sb(168, F32),
     "nl": _sb(28, U16), "nl1": _sb(32, U16), "pw": _sb(32, U16),
     "ps": ("psum", [128, 4096], F32),
 }
@@ -180,14 +180,14 @@ def rank_program(g, core, T, topo):
         do("t", lambda e: e.matmul_mx(o[0], T[ql][:, la:la + 128], T[sl][:, la:la + 128], T[qr][:, a:b], T[sr][:, a:b], True, True), o,
            V(ql, la, la + 128), V(sl, la, la + 128), V(qr, a, b), V(sr, a, b))
 
-    def PS(bank, n):
-        return V("ps", 512 * bank, 512 * bank + n)
+    def PS(bank, b, a=0):
+        return V("ps", 512 * bank + a, 512 * bank + b)
 
     def node(name, a=0, b=448, o=0):
         return V(name, o + NODE + a, o + NODE + b)
 
-    def leaf(name, half, o=0):
-        return N(name, o + (0 if half else WIN - 8 * 224), 224, 8)
+    def leaf(name, a, b, o=0):
+        return N(name, o + (8 * (a - 224)) % WIN, b - a, 8)
 
     def W(name, off, c=0, d=28, o=0):
         return I(name, o, o + WIN, off, c, d)
@@ -197,6 +197,9 @@ def rank_program(g, core, T, topo):
 
     def R(t):
         return N(t, 40, 28, 48)
+
+    def LR(t):
+        return N(t, 16, 56, 24)
 
     def swap1(t):
         tr(V("xx", 16, 80), N(t, 16, 64, 24))
@@ -210,30 +213,42 @@ def rank_program(g, core, T, topo):
     def D(name, i):
         return N(name, i, 28, 6)
 
-    def scores(half):
-        a = 224 * half
-        mm(4 + half, 224, "qa", "sa", 0, "qx", "sx", a, a + 224)
-        mm(6 + half, 224, "qb", "sb", 0, "qx", "sx", a, a + 224)
+    HALVES = ((0, 224), (224, 448))
+    SA, BA, ST, BT, KB, KD, KU, KI, KP = [V("kbo", 32 * j, 32 * j + 1) for j in range(9)]
+    SL, B3, BS = [V("kt", j, j + 1) for j in range(3)]
 
-    SA, BA, ST, BT, KB = [V("kbo", 32 * j, 32 * j + 1) for j in range(5)]
-    SL, B3 = V("kt", 4, 5), V("kt", 5, 6)
+    def scores(bank, q, s, a, b):
+        mm(bank, b - a, "qa", "sa", 0, q, s, a, b)
+        mm(bank + 2, b - a, "qb", "sb", 0, q, s, a, b)
 
-    def signs(half):
-        a = 224 * half
-        act(node("sg", a, a + 224), PS(4 + half, 224), SIGN, SA, BA)
-        act(leaf("sg", half), PS(4 + half, 224), SIGN, SL, BA)
+    def signs(bank, a, b, o=0):
+        act(node("sg", a, b), PS(bank, o + b - a, o), SIGN, SA, BA)
+        act(leaf("sg", a, b), PS(bank, o + b - a, o), SIGN, SL, BA)
 
-    def own_tests(half):
-        a = 224 * half
-        ts(V("th", a, a + 224), PS(6 + half, 224), ST, BT, MUL, GE)
+    def own_tests(q, bank, a, b, o=0):
+        if q == "v":
+            ts(V("th", a, b), PS(bank + 2, o + b - a, o), ST, BT, MUL, GE)
+        else:
+            act(V("th", a, b), PS(bank + 2, o + b - a, o), SIGN, ST, BS)
 
-    def child_steps(t, a, b):
-        tt(D("da", 0), a, L(t), SUB)
-        tt(D("da", 3), L(t), b, SUB)
-        tt(D("da", 4), b, R(t), SUB)
+    def child_steps():
+        a, b = V("ta", 5, 448, 16), V("ta", 13, 448, 16)
+        tt(D("da", 0), a, L("t0"), SUB)
+        tt(D("da", 3), L("t0"), b, SUB)
+        tt(D("da", 4), b, R("t0"), SUB)
 
-    dma("y", T.lti[:, 0:28], T.lt[:, :], writes=[("lti", range(28))])
-    dma("s", T.rti[:, 0:28], T.rt[:, :], writes=[("rti", range(28))])
+    def finish(bank, q, s, c0, a, b):
+        mm(bank, b - c0, "qv", "sv", 0, q, s, c0, b)
+        dma("y", T.oc[:, 4 * a:4 * b], T[q][:, a:b].bitcast(dt.uint8), reads=[(q, range(a, b))])
+        for k in range(4):
+            dma("y", T.osc[4 * k:4 * k + 4, a:b], T[s][32 * k:32 * k + 4, a:b], reads=[(s, range(a, b))])
+        act(V("yb", a, b), PS(bank, b - c0, a - c0))
+
+    def store_y(a, b):
+        dma("s", T.y[:, a:b], T.yb[:, a:b], reads=[("yb", range(a, b))])
+
+    dma("y", T.li[:, 0:28], T.lt[:, :], writes=[("li", range(28))])
+    dma("s", T.li[:, 28:56], T.rt[:, :], writes=[("li", range(28, 56))])
     dma("y", T.ut[:, :], T.u[:, :], writes=[("ut", range(512))])
     for h in range(2):
         dma("sy"[h], T.xa[:, 896 * h:896 * h + 896], T.x[:, 896 * h:896 * h + 896], writes=[("xa", range(896 * h, 896 * h + 896))])
@@ -248,90 +263,102 @@ def rank_program(g, core, T, topo):
         lands("lm%d" % k, 14, "aM%d" % k, p)
         lands("ql%d" % k, 224, "aC%d" % k, p)
         lands("sl%d" % k, 224, "aS%d" % k, p)
-    do("p", lambda e: e.iota(T.pi[:, 0:1], [[0, 1]], 0, 1), V("pi", 0, 1))
+    iota(V("kb", 192, 224), [[-28, 2], [-46, 16]], 30)
+    iota(V("kb", 224, 256), [[0, 2], [48, 16]], 0)
+    iota(V("kb", 256, 288), [[1, 32]], 0)
     iota(V("k1", 0, 4), [[-23, 2], [-23 * 32, 2]], SW - 16)
     iota(V("k2", 0, 4), [[24, 2], [24 * 32, 2]], 16)
-    do("p", lambda e: e.iota(T.ci[:, 0:28], [[32, 14], [0, 2]], -224, 0), V("ci", 0, 28))
-    do("p", lambda e: e.iota(T.ui[:, 0:8], [[16, 8]], 0, 0), V("ui", 0, 8))
-    for h in range(2):
-        iota(leaf("ls", h), [[1, 224]], 224 * h - 224)
-    fill(V("one", 0, 512), 1.0)
-    fill(V("kb", 0, 160), 0.0)
-    for i, (s1, s2, ops) in enumerate([(15, None, (ANDB,)), (4, 1, (SHR, ANDB)), (1, None, (ANDB,)), (31, None, (ANDB,))]):
-        ts(V("ki", i, i + 1), V("pi", 0, 1), s1, s2, *ops)
-    fill(V("xx", 0, 96), 0.0)
-    cp(V("kf", 0, 4), V("ki", 0, 4))
-    fill(node("p0"), float(NONE))
-    for j, q, s, c in [(1, 0, 1, -EPS), (0, 5, 8, -1.0), (0, 3, 8, 1.0), (0, 2, 16, 1.0), (4, 0, 4, 3.0), (4, 1, 8, 2.0), (4, 7, 8, 2.0),
-                       (1, 0, 4, EPS), (1, 1, 8, EPS), (1, 7, 8, EPS), (1, 10, 16, EPS), (3, 3, 8, 1.0), (3, 6, 8, 1.0), (3, 12, 16, 1.0),
-                       (2, 0, 8, -1.0), (2, 4, 16, -1.0), (2, 5, 8, -1.0), (2, 7, 8, -1.0), (2, 2, 8, 1.0), (2, 1, 8, 1.0)]:
-        sfill(V("kb", 32 * j + q, 32 * j + 32, s), c)
-    sfill(N("t1", 1, 512, 3), 0.0)
-    sfill(N("t0", 1, 512, 3), 0.0)
+    iota(V("ui", 0, 8), [[16, 8]], 0)
+    iota(V("ci", 0, 28), [[32, 14], [0, 2]], -224)
+    iota(node("p0"), [[0, 448]], NONE)
+    for a, b in HALVES:
+        iota(leaf("ls", a, b), [[1, 224]], a - 224)
+    fill(V("one", 0, 96), 1.0)
+    fill(V("kb", 0, 192), 0.0)
+    fill(V("one", 96, 512), 1.0)
+    rows = [(1, 0, 1, -EPS), (0, 5, 8, -1.0), (0, 3, 8, 1.0), (0, 2, 16, 1.0), (3, 3, 8, 1.0), (3, 6, 8, 1.0), (3, 12, 16, 1.0),
+            (1, 0, 4, EPS), (1, 1, 8, EPS), (1, 7, 8, EPS), (1, 10, 16, EPS), (2, 0, 8, -1.0), (2, 4, 16, -1.0), (2, 5, 8, -1.0),
+            (2, 7, 8, -1.0), (2, 2, 8, 1.0), (2, 1, 8, 1.0), (4, 0, 4, 3.0), (4, 1, 8, 2.0), (4, 7, 8, 2.0)]
 
-    def K(i):
-        return V("kt", i, i + 1)
-    X_, H_, B_ = V("kf", 0, 1), V("kf", 1, 2), V("kf", 2, 3)
-    tt(K(0), B_, H_, SUB)
-    ts(K(2), H_, -28.0, 30.0, MUL, ADD)
-    ts(K(3), X_, 48.0, None, MUL)
-    tt(K(1), K(0), K(0), MUL)
-    ts(K(2), X_, -46.0, K(2), MUL, ADD)
-    ts(V("k2", 0, 4), V("k2", 0, 4), K(3), None, ADD)
-    ts(V("k1", 0, 4), V("k1", 0, 4), K(2), K(1), ADD, MUL)
-    ts(V("nf", 0, 56, 2), V("lti", 0, 28), -224.0, None, ADD)
-    ts(V("nf", 1, 56, 2), V("rti", 0, 28), -224.0, None, ADD)
-    tt(V("k1", 0, 4), V("k1", 0, 4), V("k2", 0, 4), ADD)
-    tr(V("kbo", 0, 160), V("kb", 0, 160))
-    ts(V("n1", 0, 56), V("nf", 0, 56), 7.0, -1536.0, MUL, ADD)
-    ts(V("n2", 0, 56), V("nf", 0, 56), 224.0, None, GE)
-    ts(V("n3", 0, 56), V("nf", 0, 56), 448.0, -4096.0, GE, MUL)
-    cp(V("cl", 0, 4), V("k1", 0, 4))
-    ts(SL, SA, 0.0, None, MAX)
+    def row(how, *which):
+        for i in which:
+            j, q, s, c = rows[i]
+            how(V("kb", 32 * j + q, 32 * j + 32, s), c)
+
+    sfill(N("t1", 16, 64, 24), 0.0)
+    sfill(V("xx", 0, 96), 0.0)
+    row(sfill, *range(12))
+    sfill(V("kb", 161, 176, 2), 1.0)
+    sfill(V("kb", 176, 192, 2), 1.0)
+    sfill(N("t0", 1, 512, 3), 0.0)
+    row(fill, *range(12, 20))
+    ts(V("n1", 0, 56), V("li", 0, 56), 7.0, -3104.0, MUL, ADD)
+    ts(V("n2", 0, 56), V("li", 0, 56), 448.0, None, GE)
+    ts(V("n3", 0, 56), V("li", 0, 56), 672.0, -4096.0, GE, MUL)
+    ts(V("nf", 0, 56), V("li", 0, 56), -224.0, None, ADD)
+    tr(V("kbo", 0, 288), V("kb", 0, 288))
     tt(V("n1", 0, 56), V("n1", 0, 56), V("n2", 0, 56), MUL)
     tt(V("n3", 0, 56), V("n3", 0, 56), V("nf", 0, 56), ADD)
-    ts(V("cla", 0, 8), V("ui", 0, 8), SL, None, ADD)
+    ts(V("k1", 0, 4), V("k1", 0, 4), KU, KD, ADD, MUL)
+    ts(SL, SA, 0.0, None, MAX)
     ts(V("clb", 0, 8), V("ui", 0, 8), KB, None, ADD)
-    tt(B3, SA, SA, MUL)
-    tt(N("t1", 16, 56, 24), V("n1", 0, 56), V("n3", 0, 56), ADD)
-    swap1("t1")
+    tt(L("t1"), V("n1", 0, 28), V("n3", 0, 28), ADD)
+    tt(R("t1"), V("n1", 28, 56), V("n3", 28, 56), ADD)
+    tt(V("k1", 0, 4), V("k1", 0, 4), V("k2", 0, 4), ADD)
+    ts(V("cla", 0, 8), V("ui", 0, 8), SL, None, ADD)
     ts(V("nl", 0, 28), L("t1"), float(MID), None, ADD)
-    ts(N("t0", 7, 28, 48), V("ci", 0, 28), V("kf", 3, 4), None, ADD)
+    swap1("t1")
+    ts(V("cl", 0, 4), V("k1", 0, 4), KI, None, ADD)
+    ts(N("t0", 7, 28, 48), V("ci", 0, 28), KP, None, ADD)
+    tt(B3, SA, SA, MUL)
     swap2("t1")
     quant("qu", "su", 0, 128, "ut", 0, 512)
+    ts(BS, BT, -2.0 * EPS, EPS, MUL, ADD)
 
     def deciding(q, s, c):
         do("v", lambda e: e.tensor_copy(T[q][:, 0:128].bitcast(dt.uint32), T.qu[:, 0:128].bitcast(dt.uint32).indirect(T[c][:, 0:8])),
            V(q, 0, 128), V("qu", 0, 128), V(c, 0, 8))
         do("s", lambda e: e.activation(T[s][:, 0:128], T.su[:, 0:128].indirect(T[c][:, 0:8]), COPY), V(s, 0, 128), V("su", 0, 128), V(c, 0, 8))
 
-    for name, a, n, s in (("da", 0, 168, 1), ("db", 0, 168, 1), ("tp", 1360, 8, 24), ("tm", 1360, 8, 24), ("tg", 0, 56, 24), ("tf", 5, 56, 24)):
-        sfill(N(name, a, n, s), 0.0)
+    def unpack_tile(b):
+        do("p", lambda e: e.affine_select(T.et[:, 512 * b:512 * b + 512], T.one[:, 0:512], [[-1, 512]], AluOpType.is_equal, 0.0, b, 4),
+           V("et", 512 * b, 512 * b + 512), V("one", 0, 512))
+
+    for name in ("da", "db", "dc", "dd"):
+        sfill(V(name, 0, 168), 0.0)
+    for name, a, n in (("tp", 1360, 8), ("tm", 1360, 8), ("tg", 0, 56), ("tf", 5, 56), ("te", 3, 56)):
+        sfill(N(name, a, n, 24), 0.0)
     sfill(V("th", 448, 480), 1.0)
     for e_ in range(2):
         cp(N("t0", 16 + 24 * e_, 32, 48), I("t1", 0, TW, "cl", 2 * e_, 2 * e_ + 2))
     deciding("qa", "sa", "cla")
     tr(node("ls"), N("t0", 1, 448, 3))
     deciding("qb", "sb", "clb")
+    for a in (4, 7, 10):
+        sfill(N("t1", a, 56, 24), 0.0)
     act(node("a1"), W("ls", "nl"))
+    for b in range(2):
+        act(node("win", 0, 448, WIN * b), V("xa", b, 1792, 4), COPY, 0.5)
     for name in ("g1", "h1"):
-        for h in range(2):
-            iota(leaf(name, h), [[0, 224]], 0)
+        for a, b in HALVES:
+            iota(leaf(name, a, b), [[0, 224]], 0)
     iota(node("p1"), [[0, 448]], 0)
-    tt(D("db", 0), R("t0"), L("t0"), SUB)
+    for b in range(2):
+        unpack_tile(b)
     cp(W("p0", "nl", 0, 14), node("ls", 0, 224))
-    for h in range(2):
-        quant("qx", "sx", 224 * h, 224 * h + 224, "xa", 896 * h, 896 * h + 896)
-        scores(h)
-        signs(h)
+    for h, (a, b) in enumerate(HALVES):
+        quant("qx", "sx", a, b, "xa", 4 * a, 4 * b)
+        scores(4 + h, "qx", "sx", a, b)
+        own_tests("s", 4 + h, a, b)
+        signs(4 + h, a, b)
     cp(W("p0", "nl", 14, 28), node("ls", 224, 448))
     tr(V("ta", 0, 448), node("a1"))
     tr(N("tp", 10, 448, 3), node("p0"))
-    own_tests(0)
+    child_steps()
     swap1("tp")
-    own_tests(1)
-    swap2("tp")
     tt(D("db", 3), N("tp", 49, 28, 48), R("t0"), SUB)
+    tt(D("db", 0), R("t0"), L("t0"), SUB)
+    swap2("tp")
     pick("pw", "tp", 2, 224)
 
     xs, nl = ["xa", "xb"], "nl"
@@ -339,58 +366,68 @@ def rank_program(g, core, T, topo):
         last = k == 2
         p = T.cores[rank ^ ROUNDS[k]]
         old, new = xs[k % 2], xs[(k + 1) % 2]
-        act(V("g3", 0, 448), I("th", 0, 480, "pw", 0, 28), RELU, SA, B3)
+
+        def constants(b):
+            if k == 0:
+                quant("qe", "se", 128 * b, 128 * b + 128, "et", 512 * b, 512 * b + 512)
+        act(V("g3", 0, 448), I("th", 0, 480, "pw", 0, 28), SIGN, SA, B3)
         tt(node("g1"), W("sg", nl), V("th", 0, 448), GT)
-        child_steps("t0", V("ta", 5, 448, 16), V("ta", 13, 448, 16))
+        if k:
+            child_steps()
         act(V("g2", 0, 448), W("g1", nl), COPY, SA)
-        for h in range(2):
-            gcopy(leaf("wq", h), node("g1", 224 * h, 224 * h + 224))
+        for a, b in HALVES:
+            gcopy(leaf("wq", a, b), node("g1", a, b))
         if k == 0:
-            for b in range(4):
-                do("p", lambda e: e.affine_select(T.et[:, 512 * b:512 * b + 512], T.one[:, 0:512], [[-1, 512]], AluOpType.is_equal, 0.0, b, 4),
-                   V("et", 512 * b, 512 * b + 512), V("one", 0, 512))
+            unpack_tile(2)
+            unpack_tile(3)
         if k == 1:
             iota(node("nm"), [[1, 448]], 0)
-            for h in range(2):
-                iota(leaf("nm", h), [[1, 224]], 448 + 224 * h)
-        tr(N("tg", 1, 448, 3), V("g3", 0, 448))
-        tr(N("tg", 2, 448, 3), node("g1"))
+            for a, b in HALVES:
+                iota(leaf("nm", a, b), [[1, 224]], 448 + a)
+        for i in ((1, 2) if k else (2, 1)):
+            tr(N("tg", i, 448, 3), V("g3", 0, 448) if i == 1 else node("g1"))
+        constants(0)
         scan(V("ob", 0, 168), N("tg", 0, 168, 8), V("db", 0, 168))
         for o, i, s in ((1, 2, 12), (19, 5, 24), (22, 23, 24)):
             act(V("t1", o, 1344, s), V("tg", i, 1344, s))
-        tt(V("da", 2, 168, 3), V("ob", 2, 168, 3), N("t0", 16, 56, 24), ADD)
+        tt(V("da", 2, 168, 3), V("ob", 2, 168, 3), LR("t0"), ADD)
         tr(N("tg", 0, 448, 3), V("g2", 0, 448))
+        constants(1)
         scan(N("t1", 0, 168, 8), N("tg", 1, 168, 8), V("da", 0, 168))
-        for b in range(4):
+        for b in range(2 if k == 0 else 0, 4):
             act(node("win", 0, 448 if k == 0 else 224, WIN * b), V(old, b, 1792 if k == 0 else 896, 4), COPY, 0.5)
         swap1("t1")
         tr(node("wq"), N("t1", 1, 448, 3))
         swap2("t1")
-        tt(D("db", 0), R("t1"), L("t1"), SUB)
+        tt(D("dc", 0), R("t1"), L("t1"), SUB)
+        cp(V("dc", 2, 168, 3), LR("t1"))
         pick("nl1", "t1", 2, MID)
+        tt(D("dc", 0), D("dc", 0), N("tg", 5, 28, 48), MUL)
         act(node("h1"), W("wq", "nl1"))
-        act(V("h2", 0, 448), W("h1", "nl1"), ActivationFunctionType.Abs, ST)
+        act(V("h2", 0, 448), W("h1", "nl1"), ABS, ST)
         cp(W("p1", "nl1"), node("wq"))
-        for b in range(4):
-            if k == 0:
-                for h in range(2):
-                    act(leaf("win", h, WIN * b), V("lvt", 896 * h + b, 896 * h + 896, 4), COPY, 0.5)
-            else:
-                act(leaf("win", 0, WIN * b), PS(b, 224), COPY, 0.5)
         if not last:
             iota(node("p0"), [[0, 448]], NONE)
         tr(N("tf", 1, 448, 3), node("h1"))
+        act(N("tf", 37, 28, 48), N("tg", 5, 28, 48))
+        for b in range(4):
+            if k == 0:
+                for c0, c1 in HALVES:
+                    act(leaf("win", c0, c1, WIN * b), V("lvt", 4 * c0 + b, 4 * c1, 4), COPY, 0.5)
+            else:
+                act(leaf("win", 0, 224, WIN * b), PS(b, 224), COPY, 0.5)
         tr(N("tf", 0, 448, 3), node("p1"))
-        tt(N("tf", 19, 56, 24), N("tf", 19, 56, 24), N("tg", 23, 56, 24), MUL)
-        tt(D("da", 0), L("tf"), L("t1"), SUB)
-        tt(N("tf", 21, 56, 24), N("tf", 21, 56, 24), N("tg", 5, 56, 24), MUL)
-        tt(D("db", 3), N("tf", 39, 28, 48), R("t1"), SUB)
-        tt(D("da", 3), L("t1"), R("tf"), SUB)
-        tt(D("da", 4), R("tf"), R("t1"), SUB)
-        scan(V("ob", 0, 168), N("tf", 5, 168, 8), V("db", 0, 168))
-        tt(V("da", 2, 168, 3), V("ob", 2, 168, 3), N("t1", 16, 56, 24), ADD)
-        tr(N("tf", 11, 448, 3), V("h2", 0, 448))
-        scan(N("t0", 0, 168, 8), N("tf", 3, 168, 8), V("da", 0, 168))
+        tt(N("te", 19, 56, 24), N("tf", 19, 56, 24), N("tg", 23, 56, 24), MUL)
+        tt(D("dd", 0), L("tf"), L("t1"), SUB)
+        tt(D("dc", 3), N("tf", 39, 28, 48), R("t1"), SUB)
+        tt(D("dd", 3), L("t1"), R("tf"), SUB)
+        tt(D("dd", 4), R("tf"), R("t1"), SUB)
+        tr(N("te", 11, 448, 3), V("h2", 0, 448))
+        scan(V("ob", 0, 168), N("tf", 5, 168, 8), V("dc", 0, 168))
+        scan(V("oa", 0, 168), N("te", 3, 168, 8), V("dd", 0, 168))
+        constants(2)
+        tt(LR("t0"), V("ob", 2, 168, 3), V("oa", 2, 168, 3), ADD)
+        constants(3)
         nl, mu, lm = "rc%d" % k, "mu%d" % k, "lm%d" % k
         swap1("t0")
         tr(node("ls"), N("t0", 1, 448, 3))
@@ -423,10 +460,18 @@ def rank_program(g, core, T, topo):
             else:
                 ts(o, i, 0.03125, None, MUL)
 
+        done = [0]
+
+        def parents(n):
+            a, b = done[0], min(28, done[0] + n)
+            done[0] = b
+            if not last and b > a:
+                cp(W("p0", nl, a, b), node("ls", 16 * a, 16 * b))
+
         zr(0)
         cp(node("a1"), W("ls", nl))
-        for i in range(2):
-            gcopy(leaf("a1", i), node("a1", 224 * i, 224 * i + 224))
+        for a, b in HALVES:
+            gcopy(leaf("a1", a, b), node("a1", a, b))
         zr(1)
         act(V("ms", 0, 448), W("a1", "lr%d" % k))
         for b in range(4):
@@ -435,13 +480,8 @@ def rank_program(g, core, T, topo):
         layer(0)
         for b in range(1, 4):
             zt(1, b)
-        if k == 0:
-            tr(V("ta", 0, 448), node("a1"))
-            layer(1)
-            quant("qe", "se", 0, 512, "et", 0, 2048)
         tr(N("tm", 10, 448, 3), V("ms", 0, 448))
-        if k > 0:
-            layer(1)
+        layer(1)
         swap1("tm")
         hw(0, 0, "v")
         swap2("tm")
@@ -453,71 +493,59 @@ def rank_program(g, core, T, topo):
         for b in range(1, 4):
             hw(1, b, "vs"[b % 2])
         for b in range(4):
-            o, w = V("sh", b, 896, 4), I("hw", 448 * b, 448 * b + 448, mu, 0, 14)
-            if b % 2:
-                act(o, w)
-            else:
-                cp(o, w)
+            (act if b % 2 else cp)(V("sh", b, 896, 4), I("hw", 448 * b, 448 * b + 448, mu, 0, 14))
         qs, ss, ql, sl = "qs%d" % k, "ss%d" % k, "ql%d" % k, "sl%d" % k
+        parents(2)
         quant(qs, ss, 0, 224, "sh", 0, 896)
         send(p, T[ql][:, 0:224].bitcast(dt.uint8), T[qs][:, 0:224].bitcast(dt.uint8), "aC%d" % k, V(qs, 0, 224))
         send(p, T[sl][:, 0:224], T[ss][:, 0:224], "aS%d" % k, V(ss, 0, 224))
         if not last:
             iota(node("p1"), [[0, 448]], 0)
-            cp(W("p0", nl, 0, 14), node("ls", 0, 224))
         for b in range(4):
+            parents((14, 0, 0, 28)[b])
             tt(V(new, 896 + b, 1792, 4), I("hw", 448 * b, 448 * b + 448, lm, 0, 14), V(old, 896 + b, 1792, 4), ADD)
         if not last:
-            cp(W("p0", nl, 14, 18), node("ls", 224, 288))
+            tr(N("tp", 10, 448, 3), node("p0"))
         quant("qx", "sx", 224, 448, new, 896, 1792)
-        if not last:
-            cp(W("p0", nl, 18, 28), node("ls", 288, 448))
-            for b in range(4):
-                mm(b, 224, "qe", "se", 128 * b, ql, sl, 0, 224)
-            scores(1)
-            for b in range(4):
-                act(leaf("win", 1, WIN * b), I("hw", 448 * b, 448 * b + 448, lm, 0, 14), COPY, 0.5)
-            for b in range(4):
-                act(node("win", 224, 448, WIN * b), V(new, 896 + b, 1792, 4), COPY, 0.5)
-            signs(1)
-        else:
+        if last:
             for i in range(2):
                 act(V("gl", 448 * i, 448 * i + 448), W("nm", nl, 32 * i, 32 * i + 28))
             dma("y", T.gr[:, :], T.gl[0:128:16, 0:896], reads=[("gl", range(896))])
             quant("qv", "sv", 0, 128, "vt", 0, 512)
-            finish(mm, act, dma, V, PS, T, 1)
-            for b in range(4):
-                mm(b, 224, "qe", "se", 128 * b, ql, sl, 0, 224)
+            finish(7, "qx", "sx", 224, 224, 448)
+            store_y(224, 448)
         for b in range(4):
-            tt(V(new, b, 896, 4), V(old, b, 896, 4), PS(b, 224), ADD)
+            mm(b, 224, "qe", "se", 128 * b, ql, sl, 0, 224)
         if not last:
-            tr(N("tp", 10, 448, 3), node("p0"))
-        quant("qx", "sx", 0, 224, new, 0, 896)
-        if not last:
-            scores(0)
-            signs(0)
+            scores(5, "qx", "sx", 224, 448)
+            for b in range(4):
+                act(leaf("win", 224, 448, WIN * b), I("hw", 448 * b, 448 * b + 448, lm, 0, 14), COPY, 0.5)
+            for b in range(4):
+                act(node("win", 224, 448, WIN * b), V(new, 896 + b, 1792, 4), COPY, 0.5)
+            signs(5, 224, 448)
+            own_tests("s", 5, 224, 448)
+        for b, c0, c1 in FAR:
+            tt(V(new, 4 * c0 + b, 4 * c1, 4), V(old, 4 * c0 + b, 4 * c1, 4), PS(b, c1, c0), ADD)
+        for bank, q, s, c0, a in ((4, "qx", "sx", 0, 0), (5, "qz", "sz", 96, 128)):
+            quant(q, s, c0, c0 + 128, new, 4 * c0, 4 * c0 + 512)
+            if last:
+                finish(bank, q, s, c0, a, c0 + 128)
+            else:
+                scores(bank, q, s, c0, c0 + 128)
+                signs(bank, a, c0 + 128, a - c0)
+        if last:
+            store_y(0, 128)
+            store_y(128, 224)
+        else:
             swap1("tp")
-            if k > 0:
-                tr(V("ta", 0, 448), node("a1"))
-            own_tests(1)
+            tr(V("ta", 0, 448), node("a1"))
             swap2("tp")
             tt(D("db", 3), N("tp", 49, 28, 48), R("t0"), SUB)
+            own_tests("v", 4, 0, 128)
             pick("pw", "tp", 2, 224)
-            own_tests(0)
-        else:
-            finish(mm, act, dma, V, PS, T, 0)
+            own_tests("v", 5, 128, 224, 32)
     for q in "vstp":
         wait("y", ENG_SEM[q], cnt[q])
     for i in range(ndma[0]):
         wait("y", "d%d" % i, 16)
     g.wait_ge(T.sem["loc"], nloc[0])
-
-
-def finish(mm, act, dma, V, PS, T, half):
-    a, b = 224 * half, 224 * half + 224
-    mm(4 + half, 224, "qv", "sv", 0, "qx", "sx", a, b)
-    dma("y", T.oc[:, 4 * a:4 * b], T.qx[:, a:b].bitcast(dt.uint8), reads=[("qx", range(a, b))])
-    for k in range(4):
-        dma("y", T.osc[4 * k:4 * k + 4, a:b], T.sx[32 * k:32 * k + 4, a:b], reads=[("sx", range(a, b))])
-    act(V("yb", a, b), PS(4 + half, 224))
-    dma("s", T.y[:, a:b], T.yb[:, a:b], reads=[("yb", range(a, b))])

from concourse.mybir import dt, AluOpType, ActivationFunctionType

ROUNDS = [1, 2, 3]
PARTS = [(0, 320), (320, 448)]
FAR = [(0, 0, 224)] + [(b, 0, 128) for b in (1, 2, 3)] + [(b, 128, 224) for b in (1, 2, 3)]
ADD, SUB, MUL = AluOpType.add, AluOpType.subtract, AluOpType.mult
GE, GT, MAX = AluOpType.is_ge, AluOpType.is_gt, AluOpType.max
COPY, ABS, SIGN = ActivationFunctionType.Copy, ActivationFunctionType.Abs, ActivationFunctionType.Sign
F32, BF, I32, U16, U8, MXC = "float32", "bfloat16", "int32", "uint16", "uint8", "float8_e4m3fn_x4"
EPS = 2.0 ** -93
WIN, MID = 4096, 2048
NODE = MID - 224
NONE = 240
SW = 1536
TW = SW + 96


def _sb(n, d):
    return ("sbuf", [128, n], d)


SCRATCH = {
    "xa": _sb(1792, BF), "xb": _sb(1792, BF), "lvt": _sb(1792, BF), "ut": _sb(512, BF), "vt": _sb(512, BF),
    "one": _sb(512, BF), "et": _sb(2048, BF), "win": _sb(4 * WIN, BF), "zr": _sb(1792, BF), "zt": _sb(1792, BF),
    "hw": _sb(1792, BF), "sh": _sb(896, BF), "yb": _sb(448, F32),
    "qu": _sb(128, MXC), "su": _sb(128, U8), "qa": _sb(128, MXC), "sa": _sb(128, U8), "qb": _sb(128, MXC), "sb": _sb(128, U8),
    "qv": _sb(128, MXC), "sv": _sb(128, U8),
    "qe": _sb(512, MXC), "se": _sb(512, U8), "qw": _sb(512, MXC), "sw": _sb(512, U8), "qx": _sb(448, MXC), "sx": _sb(448, U8),
    "qz": _sb(448, MXC), "sz": _sb(448, U8),
    "li": _sb(56, I32), "ci": _sb(28, F32), "ui": _sb(8, F32),
    "kt": _sb(4, F32), "k1": _sb(4, F32), "k2": _sb(4, F32), "cl": _sb(4, U16), "cla": _sb(8, U16), "clb": _sb(8, U16),
    "kb": _sb(288, F32), "kbo": _sb(288, F32),
    "nf": _sb(56, F32), "n1": _sb(56, F32), "n2": _sb(56, F32), "n3": _sb(56, F32),
    "sg": _sb(WIN, BF), "th": _sb(480, BF), "g1": _sb(WIN, BF), "wq": _sb(WIN, BF), "h1": _sb(WIN, BF), "ls": _sb(WIN, BF),
    "a1": _sb(WIN, BF), "p0": _sb(WIN, BF), "p1": _sb(WIN, BF), "nm": _sb(WIN, F32),
    "g2": _sb(448, BF), "g3": _sb(448, BF), "h2": _sb(448, BF), "ms": _sb(448, BF), "gl": _sb(896, F32),
    "t0": _sb(TW, BF), "t1": _sb(TW, BF), "tp": _sb(TW, BF), "tm": _sb(TW, BF), "tg": _sb(1344, BF), "tf": _sb(1344, BF), "te": _sb(1360, BF), "ta": _sb(448, BF),
    "xx": _sb(96, BF), "da": _sb(168, F32), "db": _sb(168, F32), "dc": _sb(168, F32), "dd": _sb(168, F32), "oa": _sb(168, F32), "ob": _sb(168, F32),
    "nl": _sb(28, U16), "nl1": _sb(32, U16), "pw": _sb(32, U16),
    "ps": ("psum", [128, 4096], F32),
}
for _k in range(3):
    SCRATCH.update({"rc%d" % _k: _sb(64, U16), "mu%d" % _k: _sb(32, U16), "lr%d" % _k: _sb(28, U16), "lm%d" % _k: _sb(14, U16),
                    "qs%d" % _k: _sb(224, MXC), "ss%d" % _k: _sb(224, U8), "ql%d" % _k: _sb(224, MXC), "sl%d" % _k: _sb(224, U8)})
ENG_SEM = {"v": "eV", "s": "eS", "t": "eT", "p": "eP"}
SEMAPHORES = list(ENG_SEM.values()) + ["loc"] + ["d%d" % i for i in range(32)] + ["%s%d" % (a, k) for a in ("aR", "aM", "aC", "aS") for k in range(3)]


def rank_program(g, core, T, topo):
    rank = T.rank_of(core)
    if rank is None:
        return
    eng = {"v": g.vector, "s": g.scalar, "t": g.tensor, "p": g, "y": g.sync}
    cnt = {"v": 0, "s": 0, "t": 0, "p": 0}
    know = {q: {} for q in eng}
    snap, recs, ndma, nloc = {}, {}, [0], [0]

    def wait(q, sem, val):
        if know[q].get(sem, 0) >= val:
            return
        eng[q].wait_ge(T.sem[sem], val)
        for s, n in snap.get((sem, val), {}).items():
            know[q][s] = max(know[q].get(s, 0), n)
        know[q][sem] = max(know[q].get(sem, 0), val)

    def need(q, src, reads, writes):
        w = {}
        for acc, wr in [(a, False) for a in reads] + [(a, True) for a in writes]:
            name, cols = acc
            for rn, rcols, rwr, rsrc, sem, val in recs.get(name, []):
                if name == "ps":
                    if rsrc == src or not (cols & rcols):
                        continue
                elif not (wr or rwr) or not (cols & rcols):
                    continue
                w[sem] = max(w.get(sem, 0), val)
        for sem in sorted(w):
            wait(q, sem, w[sem])

    def note(src, sem, val, reads, writes):
        for name, cols in writes:
            recs[name] = [r for r in recs.get(name, []) if not (r[1] <= cols)]
        for name, cols in reads:
            recs[name] = [r for r in recs.get(name, []) if not (not r[2] and r[3] == src and src != "dma" and r[1] <= cols)]
        for acc, wr in [(a, False) for a in reads] + [(a, True) for a in writes]:
            recs.setdefault(acc[0], []).append((acc[0], acc[1], wr, src, sem, val))

    def acc(*views):
        out = []
        for v in views:
            for name, cols in v[1]:
                if name == "ps":
                    cols = frozenset(x // 512 for x in cols)
                out.append((name, frozenset(cols)))
        return out

    def V(name, a, b, s=1):
        return (T[name][:, a:b] if s == 1 else T[name][:, a:b:s], [(name, range(a, b, s))])

    def N(name, a, n, s):
        return V(name, a, a + (n - 1) * s + 1, s)

    def I(name, a, b, off, c, d):
        return (T[name][:, a:b].indirect(T[off][:, c:d]), [(name, range(a, b)), (off, range(c, d))])

    def do(q, call, out, *ins):
        outs = list(out) if isinstance(out, list) else [out]
        reads, writes = [], acc(*[(o[0], o[1][:1]) for o in outs])
        for o in outs:
            reads += acc((None, o[1][1:]))
        reads += acc(*ins)
        need(q, q, reads, writes)
        r = call(eng[q])
        cnt[q] += 1
        sem = ENG_SEM[q]
        r.then_inc(T.sem[sem], 1)
        k = dict(know[q])
        k[sem] = cnt[q]
        snap[(sem, cnt[q])] = k
        note(q, sem, cnt[q], reads, writes)

    def dma(q, out_ap, in_ap, reads=(), writes=()):
        need(q, "dma", acc((None, reads)), acc((None, writes)))
        sem = "d%d" % ndma[0]
        ndma[0] += 1
        eng[q].dma_start(out_ap, in_ap).then_inc(T.sem[sem], 16)
        snap[(sem, 16)] = dict(know[q])
        note("dma", sem, 16, acc((None, reads)), acc((None, writes)))

    def send(dst, out_ap, in_ap, sem, view):
        need("p", "rem", acc(view), [])
        a = topo.addr(dst)
        g.remote_dma(out_ap, in_ap, T.sem[sem], T.sem["loc"], a[1], a[0], topo.mask(core, dst))
        nloc[0] += len(topo.engines(core, dst))

    def lands(name, n, sem, src):
        recs.setdefault(name, []).append((name, frozenset(range(n)), True, "rem", sem, len(topo.engines(src, core))))

    def tt(out, a, b, op):
        do("v", lambda e: e.tensor_tensor(out[0], a[0], b[0], op), out, a, b)

    def ts(out, a, s1, s2, op0, *op1):
        sc = [x for x in (s1, s2) if isinstance(x, tuple)]
        do("v", lambda e: e.tensor_scalar(out[0], a[0], s1[0] if isinstance(s1, tuple) else s1, s2[0] if isinstance(s2, tuple) else s2, op0, *op1), out, a, *sc)

    def cp(out, a):
        do("v", lambda e: e.tensor_copy(out[0], a[0]), out, a)

    def tr(out, a):
        do("v", lambda e: e.transpose(out[0], a[0]), out, a)

    def fill(out, c):
        do("v", lambda e: e.memset(out[0], c), out)

    def scan(out, d0, d1):
        do("v", lambda e: e.tensor_tensor_scan(out[0], d0[0], d1[0], 0.0, MUL, ADD), out, d0, d1)

    def act(out, a, func=COPY, scale=1.0, bias=None):
        col = [x for x in (scale, bias) if isinstance(x, tuple)]
        sc = scale[0] if isinstance(scale, tuple) else scale
        if bias is None:
            do("s", lambda e: e.activation(out[0], a[0], func, scale=sc), out, a, *col)
        else:
            do("s", lambda e: e.activation(out[0], a[0], func, bias=bias[0], scale=sc), out, a, *col)

    def sfill(out, c):
        act(out, V("one", 0, len(out[1][0][1])), COPY, c)

    def iota(out, pattern, base, cm=0):
        do("p", lambda e: e.iota(out[0], pattern, base, cm, allow_small_or_imprecise_dtypes=True), out)

    def gcopy(out, a):
        do("p", lambda e: e.affine_select(out[0], a[0], [[0, len(out[1][0][1])]], GE, 0.0, 0, 0), out, a)

    def quant(q, s, a, b, tile, ta, tb):
        do("v", lambda e: e.quantize_mx(T[q][:, a:b], T[s][:, a:b], T[tile][:, ta:tb]), [V(q, a, b), V(s, a, b)], V(tile, ta, tb))

    def mm(bank, n, ql, sl, la, qr, sr, a, b):
        o = V("ps", 512 * bank, 512 * bank + n)
        do("t", lambda e: e.matmul_mx(o[0], T[ql][:, la:la + 128], T[sl][:, la:la + 128], T[qr][:, a:b], T[sr][:, a:b], True, True), o,
           V(ql, la, la + 128), V(sl, la, la + 128), V(qr, a, b), V(sr, a, b))

    def PS(bank, b, a=0):
        return V("ps", 512 * bank + a, 512 * bank + b)

    def node(name, a=0, b=448, o=0):
        return V(name, o + NODE + a, o + NODE + b)

    def leaf(name, a, b, o=0):
        return N(name, o + (8 * (a - 224)) % WIN, b - a, 8)

    def W(name, off, c=0, d=28, o=0):
        return I(name, o, o + WIN, off, c, d)

    def L(t):
        return N(t, 16, 28, 48)

    def R(t):
        return N(t, 40, 28, 48)

    def LR(t):
        return N(t, 16, 56, 24)

    def swap1(t):
        tr(V("xx", 16, 80), N(t, 16, 64, 24))

    def swap2(t):
        tr(V(t, SW, TW), V("xx", 0, 96))

    def pick(out, t, n, add):
        ts(V(out, 0, 16 * n), I(t, 0, TW, "cl", 0, n), float(add), None, ADD)

    def D(name, i):
        return N(name, i, 28, 6)

    HALVES = ((0, 224), (224, 448))
    SA, BA, ST, BT, KB, KD, KU, KI, KP = [V("kbo", 32 * j, 32 * j + 1) for j in range(9)]
    SL, B3, BS = [V("kt", j, j + 1) for j in range(3)]

    def scores(bank, q, s, a, b):
        mm(bank, b - a, "qa", "sa", 0, q, s, a, b)
        mm(bank + 2, b - a, "qb", "sb", 0, q, s, a, b)

    def signs(bank, a, b, o=0):
        act(node("sg", a, b), PS(bank, o + b - a, o), SIGN, SA, BA)
        act(leaf("sg", a, b), PS(bank, o + b - a, o), SIGN, SL, BA)

    def own_tests(q, bank, a, b, o=0):
        if q == "v":
            ts(V("th", a, b), PS(bank + 2, o + b - a, o), ST, BT, MUL, GE)
        else:
            act(V("th", a, b), PS(bank + 2, o + b - a, o), SIGN, ST, BS)

    def child_steps():
        a, b = V("ta", 5, 448, 16), V("ta", 13, 448, 16)
        tt(D("da", 0), a, L("t0"), SUB)
        tt(D("da", 3), L("t0"), b, SUB)
        tt(D("da", 4), b, R("t0"), SUB)

    def finish(bank, q, s, c0, a, b):
        mm(bank, b - c0, "qv", "sv", 0, q, s, c0, b)
        dma("y", T.oc[:, 4 * a:4 * b], T[q][:, a:b].bitcast(dt.uint8), reads=[(q, range(a, b))])
        for k in range(4):
            dma("y", T.osc[4 * k:4 * k + 4, a:b], T[s][32 * k:32 * k + 4, a:b], reads=[(s, range(a, b))])
        act(V("yb", a, b), PS(bank, b - c0, a - c0))

    def store_y(a, b):
        dma("s", T.y[:, a:b], T.yb[:, a:b], reads=[("yb", range(a, b))])

    dma("y", T.li[:, 0:28], T.lt[:, :], writes=[("li", range(28))])
    dma("s", T.li[:, 28:56], T.rt[:, :], writes=[("li", range(28, 56))])
    dma("y", T.ut[:, :], T.u[:, :], writes=[("ut", range(512))])
    for h in range(2):
        dma("sy"[h], T.xa[:, 896 * h:896 * h + 896], T.x[:, 896 * h:896 * h + 896], writes=[("xa", range(896 * h, 896 * h + 896))])
    need("y", "dma", acc(V("xa", 0, 1792)), [])
    dma("y", T.lvt[:, :], T.lv[:, :], writes=[("lvt", range(1792))])
    dma("y", T.qw[:, 0:512].bitcast(dt.uint8), T.wc[:, :], writes=[("qw", range(512))])
    dma("y", T.sw[:, 0:512], T.ws[:, :], writes=[("sw", range(512))])
    dma("y", T.vt[:, :], T.v[:, :], writes=[("vt", range(512))])
    for k in range(3):
        p = T.cores[rank ^ ROUNDS[k]]
        lands("lr%d" % k, 28, "aR%d" % k, p)
        lands("lm%d" % k, 14, "aM%d" % k, p)
        lands("ql%d" % k, 224, "aC%d" % k, p)
        lands("sl%d" % k, 224, "aS%d" % k, p)
    iota(V("kb", 192, 224), [[-28, 2], [-46, 16]], 30)
    iota(V("kb", 224, 256), [[0, 2], [48, 16]], 0)
    iota(V("kb", 256, 288), [[1, 32]], 0)
    iota(V("k1", 0, 4), [[-23, 2], [-23 * 32, 2]], SW - 16)
    iota(V("k2", 0, 4), [[24, 2], [24 * 32, 2]], 16)
    iota(V("ui", 0, 8), [[16, 8]], 0)
    iota(V("ci", 0, 28), [[32, 14], [0, 2]], -224)
    iota(node("p0"), [[0, 448]], NONE)
    for a, b in HALVES:
        iota(leaf("ls", a, b), [[1, 224]], a - 224)
    fill(V("one", 0, 96), 1.0)
    fill(V("kb", 0, 192), 0.0)
    fill(V("one", 96, 512), 1.0)
    rows = [(1, 0, 1, -EPS), (0, 5, 8, -1.0), (0, 3, 8, 1.0), (0, 2, 16, 1.0), (3, 3, 8, 1.0), (3, 6, 8, 1.0), (3, 12, 16, 1.0),
            (1, 0, 4, EPS), (1, 1, 8, EPS), (1, 7, 8, EPS), (1, 10, 16, EPS), (2, 0, 8, -1.0), (2, 4, 16, -1.0), (2, 5, 8, -1.0),
            (2, 7, 8, -1.0), (2, 2, 8, 1.0), (2, 1, 8, 1.0), (4, 0, 4, 3.0), (4, 1, 8, 2.0), (4, 7, 8, 2.0)]

    def row(how, *which):
        for i in which:
            j, q, s, c = rows[i]
            how(V("kb", 32 * j + q, 32 * j + 32, s), c)

    sfill(N("t1", 16, 64, 24), 0.0)
    sfill(V("xx", 0, 96), 0.0)
    row(sfill, *range(12))
    sfill(V("kb", 161, 176, 2), 1.0)
    sfill(V("kb", 176, 192, 2), 1.0)
    sfill(N("t0", 1, 512, 3), 0.0)
    row(fill, *range(12, 20))
    ts(V("n1", 0, 56), V("li", 0, 56), 7.0, -3104.0, MUL, ADD)
    ts(V("n2", 0, 56), V("li", 0, 56), 448.0, None, GE)
    ts(V("n3", 0, 56), V("li", 0, 56), 672.0, -4096.0, GE, MUL)
    ts(V("nf", 0, 56), V("li", 0, 56), -224.0, None, ADD)
    tr(V("kbo", 0, 288), V("kb", 0, 288))
    tt(V("n1", 0, 56), V("n1", 0, 56), V("n2", 0, 56), MUL)
    tt(V("n3", 0, 56), V("n3", 0, 56), V("nf", 0, 56), ADD)
    ts(V("k1", 0, 4), V("k1", 0, 4), KU, KD, ADD, MUL)
    ts(SL, SA, 0.0, None, MAX)
    ts(V("clb", 0, 8), V("ui", 0, 8), KB, None, ADD)
    tt(L("t1"), V("n1", 0, 28), V("n3", 0, 28), ADD)
    tt(R("t1"), V("n1", 28, 56), V("n3", 28, 56), ADD)
    tt(V("k1", 0, 4), V("k1", 0, 4), V("k2", 0, 4), ADD)
    ts(V("cla", 0, 8), V("ui", 0, 8), SL, None, ADD)
    ts(V("nl", 0, 28), L("t1"), float(MID), None, ADD)
    swap1("t1")
    ts(V("cl", 0, 4), V("k1", 0, 4), KI, None, ADD)
    ts(N("t0", 7, 28, 48), V("ci", 0, 28), KP, None, ADD)
    tt(B3, SA, SA, MUL)
    swap2("t1")
    quant("qu", "su", 0, 128, "ut", 0, 512)
    ts(BS, BT, -2.0 * EPS, EPS, MUL, ADD)

    def deciding(q, s, c):
        do("v", lambda e: e.tensor_copy(T[q][:, 0:128].bitcast(dt.uint32), T.qu[:, 0:128].bitcast(dt.uint32).indirect(T[c][:, 0:8])),
           V(q, 0, 128), V("qu", 0, 128), V(c, 0, 8))
        do("s", lambda e: e.activation(T[s][:, 0:128], T.su[:, 0:128].indirect(T[c][:, 0:8]), COPY), V(s, 0, 128), V("su", 0, 128), V(c, 0, 8))

    def unpack_tile(b):
        do("p", lambda e: e.affine_select(T.et[:, 512 * b:512 * b + 512], T.one[:, 0:512], [[-1, 512]], AluOpType.is_equal, 0.0, b, 4),
           V("et", 512 * b, 512 * b + 512), V("one", 0, 512))

    for name in ("da", "db", "dc", "dd"):
        sfill(V(name, 0, 168), 0.0)
    for name, a, n in (("tp", 1360, 8), ("tm", 1360, 8), ("tg", 0, 56), ("tf", 5, 56), ("te", 3, 56)):
        sfill(N(name, a, n, 24), 0.0)
    sfill(V("th", 448, 480), 1.0)
    for e_ in range(2):
        cp(N("t0", 16 + 24 * e_, 32, 48), I("t1", 0, TW, "cl", 2 * e_, 2 * e_ + 2))
    deciding("qa", "sa", "cla")
    tr(node("ls"), N("t0", 1, 448, 3))
    deciding("qb", "sb", "clb")
    for a in (4, 7, 10):
        sfill(N("t1", a, 56, 24), 0.0)
    act(node("a1"), W("ls", "nl"))
    for b in range(2):
        act(node("win", 0, 448, WIN * b), V("xa", b, 1792, 4), COPY, 0.5)
    for name in ("g1", "h1"):
        for a, b in HALVES:
            iota(leaf(name, a, b), [[0, 224]], 0)
    iota(node("p1"), [[0, 448]], 0)
    for b in range(2):
        unpack_tile(b)
    cp(W("p0", "nl", 0, 14), node("ls", 0, 224))
    for h, (a, b) in enumerate(HALVES):
        quant("qx", "sx", a, b, "xa", 4 * a, 4 * b)
        scores(4 + h, "qx", "sx", a, b)
        own_tests("s", 4 + h, a, b)
        signs(4 + h, a, b)
    cp(W("p0", "nl", 14, 28), node("ls", 224, 448))
    tr(V("ta", 0, 448), node("a1"))
    tr(N("tp", 10, 448, 3), node("p0"))
    child_steps()
    swap1("tp")
    tt(D("db", 3), N("tp", 49, 28, 48), R("t0"), SUB)
    tt(D("db", 0), R("t0"), L("t0"), SUB)
    swap2("tp")
    pick("pw", "tp", 2, 224)

    xs, nl = ["xa", "xb"], "nl"
    for k in range(3):
        last = k == 2
        p = T.cores[rank ^ ROUNDS[k]]
        old, new = xs[k % 2], xs[(k + 1) % 2]

        def constants(b):
            if k == 0:
                quant("qe", "se", 128 * b, 128 * b + 128, "et", 512 * b, 512 * b + 512)
        act(V("g3", 0, 448), I("th", 0, 480, "pw", 0, 28), SIGN, SA, B3)
        tt(node("g1"), W("sg", nl), V("th", 0, 448), GT)
        if k:
            child_steps()
        act(V("g2", 0, 448), W("g1", nl), COPY, SA)
        for a, b in HALVES:
            gcopy(leaf("wq", a, b), node("g1", a, b))
        if k == 0:
            unpack_tile(2)
            unpack_tile(3)
        if k == 1:
            iota(node("nm"), [[1, 448]], 0)
            for a, b in HALVES:
                iota(leaf("nm", a, b), [[1, 224]], 448 + a)
        for i in ((1, 2) if k else (2, 1)):
            tr(N("tg", i, 448, 3), V("g3", 0, 448) if i == 1 else node("g1"))
        constants(0)
        scan(V("ob", 0, 168), N("tg", 0, 168, 8), V("db", 0, 168))
        for o, i, s in ((1, 2, 12), (19, 5, 24), (22, 23, 24)):
            act(V("t1", o, 1344, s), V("tg", i, 1344, s))
        tt(V("da", 2, 168, 3), V("ob", 2, 168, 3), LR("t0"), ADD)
        tr(N("tg", 0, 448, 3), V("g2", 0, 448))
        constants(1)
        scan(N("t1", 0, 168, 8), N("tg", 1, 168, 8), V("da", 0, 168))
        for b in range(2 if k == 0 else 0, 4):
            act(node("win", 0, 448 if k == 0 else 224, WIN * b), V(old, b, 1792 if k == 0 else 896, 4), COPY, 0.5)
        swap1("t1")
        tr(node("wq"), N("t1", 1, 448, 3))
        swap2("t1")
        tt(D("dc", 0), R("t1"), L("t1"), SUB)
        cp(V("dc", 2, 168, 3), LR("t1"))
        pick("nl1", "t1", 2, MID)
        tt(D("dc", 0), D("dc", 0), N("tg", 5, 28, 48), MUL)
        act(node("h1"), W("wq", "nl1"))
        act(V("h2", 0, 448), W("h1", "nl1"), ABS, ST)
        cp(W("p1", "nl1"), node("wq"))
        if not last:
            iota(node("p0"), [[0, 448]], NONE)
        tr(N("tf", 1, 448, 3), node("h1"))
        act(N("tf", 37, 28, 48), N("tg", 5, 28, 48))
        for b in range(4):
            if k == 0:
                for c0, c1 in HALVES:
                    act(leaf("win", c0, c1, WIN * b), V("lvt", 4 * c0 + b, 4 * c1, 4), COPY, 0.5)
            else:
                act(leaf("win", 0, 224, WIN * b), PS(b, 224), COPY, 0.5)
        tr(N("tf", 0, 448, 3), node("p1"))
        tt(N("te", 19, 56, 24), N("tf", 19, 56, 24), N("tg", 23, 56, 24), MUL)
        tt(D("dd", 0), L("tf"), L("t1"), SUB)
        tt(D("dc", 3), N("tf", 39, 28, 48), R("t1"), SUB)
        tt(D("dd", 3), L("t1"), R("tf"), SUB)
        tt(D("dd", 4), R("tf"), R("t1"), SUB)
        tr(N("te", 11, 448, 3), V("h2", 0, 448))
        scan(V("ob", 0, 168), N("tf", 5, 168, 8), V("dc", 0, 168))
        scan(V("oa", 0, 168), N("te", 3, 168, 8), V("dd", 0, 168))
        constants(2)
        tt(LR("t0"), V("ob", 2, 168, 3), V("oa", 2, 168, 3), ADD)
        constants(3)
        nl, mu, lm = "rc%d" % k, "mu%d" % k, "lm%d" % k
        swap1("t0")
        tr(node("ls"), N("t0", 1, 448, 3))
        swap2("t0")
        if not last:
            tt(D("db", 0), R("t0"), L("t0"), SUB)
        pick(nl, "t0", 4, MID)
        send(p, T["lr%d" % k][:, 0:28], T[nl][:, 32:60], "aR%d" % k, V(nl, 32, 60))

        def zr(h):
            c0, c1 = PARTS[h]
            for b in range(4):
                act(V("zr", 448 * b + c0, 448 * b + c1), W("win", nl, 32 + c0 // 16, 32 + c1 // 16, WIN * b))

        def zt(h, b):
            c0, c1 = PARTS[h]
            tt(V("zt", 4 * c0 + b, 4 * c1, 4), W("win", nl, c0 // 16, c1 // 16, WIN * b), V("zr", 448 * b + c0, 448 * b + c1), ADD)

        def layer(h):
            c0, c1 = PARTS[h]
            quant("qz", "sz", c0, c1, "zt", 4 * c0, 4 * c1)
            for b in range(4):
                mm(4 * h + b, c1 - c0, "qw", "sw", 128 * b, "qz", "sz", c0, c1)

        def hw(h, b, q):
            c0, c1 = PARTS[h]
            o, i = V("hw", 448 * b + c0, 448 * b + c1), PS(4 * h + b, c1 - c0)
            if q == "s":
                act(o, i, COPY, 0.03125)
            else:
                ts(o, i, 0.03125, None, MUL)

        done = [0]

        def parents(n):
            a, b = done[0], min(28, done[0] + n)
            done[0] = b
            if not last and b > a:
                cp(W("p0", nl, a, b), node("ls", 16 * a, 16 * b))

        zr(0)
        cp(node("a1"), W("ls", nl))
        for a, b in HALVES:
            gcopy(leaf("a1", a, b), node("a1", a, b))
        zr(1)
        act(V("ms", 0, 448), W("a1", "lr%d" % k))
        for b in range(4):
            zt(0, b)
        zt(1, 0)
        layer(0)
        for b in range(1, 4):
            zt(1, b)
        tr(N("tm", 10, 448, 3), V("ms", 0, 448))
        layer(1)
        swap1("tm")
        hw(0, 0, "v")
        swap2("tm")
        for b in range(1, 4):
            hw(0, b, "s")
        hw(1, 0, "v")
        pick(mu, "tm", 2, 224)
        send(p, T[lm][:, 0:14], T[mu][:, 14:28], "aM%d" % k, V(mu, 14, 28))
        for b in range(1, 4):
            hw(1, b, "vs"[b % 2])
        for b in range(4):
            (act if b % 2 else cp)(V("sh", b, 896, 4), I("hw", 448 * b, 448 * b + 448, mu, 0, 14))
        qs, ss, ql, sl = "qs%d" % k, "ss%d" % k, "ql%d" % k, "sl%d" % k
        parents(2)
        quant(qs, ss, 0, 224, "sh", 0, 896)
        send(p, T[ql][:, 0:224].bitcast(dt.uint8), T[qs][:, 0:224].bitcast(dt.uint8), "aC%d" % k, V(qs, 0, 224))
        send(p, T[sl][:, 0:224], T[ss][:, 0:224], "aS%d" % k, V(ss, 0, 224))
        if not last:
            iota(node("p1"), [[0, 448]], 0)
        for b in range(4):
            parents((14, 0, 0, 28)[b])
            tt(V(new, 896 + b, 1792, 4), I("hw", 448 * b, 448 * b + 448, lm, 0, 14), V(old, 896 + b, 1792, 4), ADD)
        if not last:
            tr(N("tp", 10, 448, 3), node("p0"))
        quant("qx", "sx", 224, 448, new, 896, 1792)
        if last:
            for i in range(2):
                act(V("gl", 448 * i, 448 * i + 448), W("nm", nl, 32 * i, 32 * i + 28))
            dma("y", T.gr[:, :], T.gl[0:128:16, 0:896], reads=[("gl", range(896))])
            quant("qv", "sv", 0, 128, "vt", 0, 512)
            finish(7, "qx", "sx", 224, 224, 448)
            store_y(224, 448)
        for b in range(4):
            mm(b, 224, "qe", "se", 128 * b, ql, sl, 0, 224)
        if not last:
            scores(5, "qx", "sx", 224, 448)
            for b in range(4):
                act(leaf("win", 224, 448, WIN * b), I("hw", 448 * b, 448 * b + 448, lm, 0, 14), COPY, 0.5)
            for b in range(4):
                act(node("win", 224, 448, WIN * b), V(new, 896 + b, 1792, 4), COPY, 0.5)
            signs(5, 224, 448)
            own_tests("s", 5, 224, 448)
        for b, c0, c1 in FAR:
            tt(V(new, 4 * c0 + b, 4 * c1, 4), V(old, 4 * c0 + b, 4 * c1, 4), PS(b, c1, c0), ADD)
        for bank, q, s, c0, a in ((4, "qx", "sx", 0, 0), (5, "qz", "sz", 96, 128)):
            quant(q, s, c0, c0 + 128, new, 4 * c0, 4 * c0 + 512)
            if last:
                finish(bank, q, s, c0, a, c0 + 128)
            else:
                scores(bank, q, s, c0, c0 + 128)
                signs(bank, a, c0 + 128, a - c0)
        if last:
            store_y(0, 128)
            store_y(128, 224)
        else:
            swap1("tp")
            tr(V("ta", 0, 448), node("a1"))
            swap2("tp")
            tt(D("db", 3), N("tp", 49, 28, 48), R("t0"), SUB)
            own_tests("v", 4, 0, 128)
            pick("pw", "tp", 2, 224)
            own_tests("v", 5, 128, 224, 32)
    for q in "vstp":
        wait("y", ENG_SEM[q], cnt[q])
    for i in range(ndma[0]):
        wait("y", "d%d" % i, 16)
    g.wait_ge(T.sem["loc"], nloc[0])
